import numpy as np
import ml_dtypes


def mxq(x, axis, fmt="e4m3"):
    dtype, down = {"e4m3": (ml_dtypes.float8_e4m3fn, 7), "e5m2": (ml_dtypes.float8_e5m2, 14)}[fmt]
    v = np.moveaxis(np.asarray(x, np.float32).astype(ml_dtypes.bfloat16).astype(np.float64), axis, -1)
    blocks = v.reshape(v.shape[:-1] + (-1, 32))
    amax = np.abs(blocks).max(-1, keepdims=True)
    byte = np.maximum(np.where(amax > 0, np.frexp(amax)[1] - 1 + 127, 0) - down, 1)
    scale = np.exp2(byte - 127.0)
    codes = (blocks / scale).astype(np.float32).astype(dtype).astype(np.float64)
    return np.moveaxis((codes * scale).reshape(v.shape), -1, axis)


WIDE = False


def mx_kscale(k):
    if not WIDE:
        return np.ones(k)
    levels = np.array([10, -10, 5, -5, 0])
    if k % 512:
        return np.exp2(np.random.permutation(np.resize(levels, k // 32))).repeat(32)
    a = np.empty((k // 512, 16))
    for p in range(k // 512):
        a[p, :8] = np.random.permutation(np.resize(levels, 8))
        for g in range(8):
            far = levels[np.abs(levels - a[p, g]) >= 10]
            a[p, g + 8] = far[np.random.randint(len(far))]
    return np.exp2(a.ravel()).repeat(32)


def f64(x):
    return np.asarray(x).astype(np.float64)


def striped(idx):
    return np.tile(idx.reshape(-1, 16).T, (8, 1)).astype(np.uint16)


def unstriped(offs):
    return offs[:16].T.reshape(-1).astype(np.int64)


def pack_weight(w):
    k, n = w.shape
    w = f64(np.asarray(w, np.float32).astype(ml_dtypes.bfloat16)).reshape(k // 32, 32, n)
    amax = np.abs(w).max(1)
    byte = np.clip(np.where(amax > 0, np.frexp(amax)[1] - 1 + 127 - 7, 1), 1, 254)
    scaled = (w * np.exp2(127.0 - byte)[:, None, :]).reshape(k, n).astype(np.float32)
    words = np.ascontiguousarray(scaled.reshape(k // 512, 128, 4, n).transpose(0, 1, 3, 2)).astype(ml_dtypes.float8_e4m3fn).view(np.uint8)
    return words, np.ascontiguousarray(byte.astype(np.uint8).reshape(k // 512, 16, n))


def unpack_weight(words, scales):
    g, p, n, _ = words.shape
    vals = np.ascontiguousarray(words).view(ml_dtypes.float8_e4m3fn).astype(np.float64) * np.repeat(np.exp2(scales.astype(np.float64) - 127.0), 8, axis=1)[..., None]
    return vals.transpose(0, 1, 3, 2).reshape(g * 512, n)


E2M1 = np.array([0.0, 0.5, 1.0, 1.5, 2.0, 3.0, 4.0, 6.0, -0.0, -0.5, -1.0, -1.5, -2.0, -3.0, -4.0, -6.0])


def pack_fp4(w):
    k, n = w.shape
    w = f64(np.asarray(w, np.float32).astype(ml_dtypes.bfloat16)).reshape(k // 32, 32, n)
    amax = np.abs(w).max(1)
    mant, ex = np.frexp(amax / 6.0)
    byte = np.clip(np.where(amax > 0, np.where(mant > 0.5, ex, ex - 1) + 127, 1), 1, 254)
    scaled = (w * np.exp2(127.0 - byte)[:, None, :]).reshape(k, n).astype(np.float32)
    c = np.ascontiguousarray(scaled.reshape(k // 512, 128, 4, n).transpose(0, 1, 3, 2)).astype(ml_dtypes.float4_e2m1fn).view(np.uint8) & 0xF
    words = (c[..., 0::2] | (c[..., 1::2] << 4)).reshape(k // 512, 128, 2 * n)
    return np.ascontiguousarray(words), np.ascontiguousarray(byte.astype(np.uint8).reshape(k // 512, 16, n))


def unpack_fp4(words, scales):
    g, _, n = scales.shape
    words = np.ascontiguousarray(words).reshape(g, 128, n, 2)
    nib = np.empty((g, 128, n, 4), np.uint8)
    nib[..., 0::2] = words & 0xF
    nib[..., 1::2] = words >> 4
    vals = E2M1[nib] * np.repeat(np.exp2(scales.astype(np.float64) - 127.0), 8, axis=1)[..., None]
    return vals.transpose(0, 1, 3, 2).reshape(g * 512, n)


def relu(v):
    return np.maximum(v, 0.0)


K, T, S, V, H, N = 512, 4096, 1024, 512, 512, 128


def setup_inputs():
    n = np.random.standard_normal
    s = mx_kscale(K)[:, None]
    u = mx_kscale(H)
    packed_xT = pack_weight(n((K, T)) * s)
    packed_w2 = pack_fp4(n((H, N)) / np.sqrt(2 * H) / u[:, None])
    packed_w3 = pack_fp4(n((H, N)) / np.sqrt(2 * H) / u[:, None])
    return {
        "x_words": packed_xT[0],
        "x_scales": packed_xT[1],
        "w1": (n((K, H)) / np.sqrt(K) / s * u).astype(np.float32),
        "w2_words": packed_w2[0],
        "w2_scales": packed_w2[1],
        "w3_words": packed_w3[0],
        "w3_scales": packed_w3[1],
        "offs": striped(np.random.permutation(T)[:S]),
        "cen": striped(np.random.permutation(S)[:V]),
        "pos1": striped(np.random.permutation(S)[:V]),
        "pos2": striped(np.random.permutation(S)[:V]),
        "pos3": striped(np.random.permutation(S)[:V]),
    }


def reference(x_words, x_scales, w1, w2_words, w2_scales, w3_words, w3_scales, offs, cen, pos1, pos2, pos3):
    xq = unpack_weight(x_words, x_scales)[:, unstriped(offs)]
    h = relu(mxq(f64(w1), 0, "e4m3").T @ xq)
    hc = h[:, unstriped(cen)]
    z = (h[:, unstriped(pos1)] + h[:, unstriped(pos2)] + h[:, unstriped(pos3)]) / 3
    return unpack_fp4(w2_words, w2_scales).T @ mxq(hc, 0, "e4m3") + unpack_fp4(w3_words, w3_scales).T @ mxq(z, 0, "e4m3")

@@ -1,0 +1,205 @@
+from contextlib import ExitStack
+
+import concourse.mybir as mybir
+from concourse.masks import make_identity
+
+K, T, S, V, H, N = 512, 4096, 1024, 512, 512, 128
+FLOPS = 2 * K * H * S + 2 * 2 * H * N * V
+
+F32 = mybir.dt.float32
+BF16 = mybir.dt.bfloat16
+I32 = mybir.dt.int32
+U32 = mybir.dt.uint32
+U16 = mybir.dt.uint16
+U8 = mybir.dt.uint8
+FP8X4 = mybir.dt.float8_e4m3fn_x4
+FP4X4 = mybir.dt.float4_e2m1fn_x4
+COPY = mybir.ActivationFunctionType.Copy
+RELU = mybir.ActivationFunctionType.Relu
+
+P = 128
+PACK = 4
+BANK = 512
+LIST_ROWS = 16
+BLOCKS = V // P
+CEN_PIECES = ((0, 256), (256, 384), (384, 512))
+
+
+def tile_picked_sagecat_mean_p_kernel(
+    tc, x_words, x_scales, w1, w2_words, w2_scales, w3_words, w3_scales, offs, cen, pos1, pos2, pos3, out
+):
+    nc = tc.nc
+    with ExitStack() as ctx:
+        keep = ctx.enter_context(tc.tile_pool(name="keep", bufs=1))
+        psum = ctx.enter_context(tc.psum_pool(name="psum", bufs=1))
+
+        def load_list(name, src):
+            tile = keep.tile(list(src.shape), U16, name=name)
+            nc.sync.dma_start(tile[:], src)
+            return tile
+
+        def load_scale_rows(queue, plane, rows):
+            for q in range(4):
+                queue.dma_start(
+                    out=plane[32 * q : 32 * q + 4, :].bitcast(I32), in_=rows[0, 4 * q : 4 * q + 4, :].bitcast(I32)
+                )
+
+        x_plane = keep.tile([P, T], U8, name="x_plane")
+        nc.vector.memset(x_plane[:].bitcast(I32), 0)
+        w2_plane = keep.tile([P, N], U8, name="w2_plane", align_bytes=64)
+        w3_plane = keep.tile([P, N], U8, name="w3_plane", align_bytes=64)
+        nc.vector.memset(w2_plane[:].bitcast(I32), 0)
+        nc.vector.memset(w3_plane[:].bitcast(I32), 0)
+
+        offs_list = load_list("offs_list", offs)
+        x_table = keep.tile([P, T], U32, name="x_table")
+        nc.sync.dma_start(out=x_table[:].bitcast(I32), in_=x_words[0].rearrange("p n t -> p (n t)").bitcast(I32))
+        load_scale_rows(nc.scalar, x_plane, x_scales)
+        w1_rows = w1.rearrange("(p j) c -> p j c", j=PACK)
+        w1_raw = []
+        for half in range(2):
+            raw = keep.tile([P, PACK, H // 2], F32, name="w1_raw%d" % half)
+            nc.sync.dma_start(out=raw[:], in_=w1_rows[:, :, half * (H // 2) : (half + 1) * (H // 2)])
+            w1_raw.append(raw)
+        pos_lists = [load_list("pos%d_list" % d, src) for d, src in enumerate((pos1, pos2, pos3))]
+        cen_list = load_list("cen_list", cen)
+        w2_codes = keep.tile([P, 2 * N], U8, name="w2_codes", align_bytes=64)
+        w3_codes = keep.tile([P, 2 * N], U8, name="w3_codes", align_bytes=64)
+        nc.sync.dma_start(out=w3_codes[:].bitcast(I32), in_=w3_words[0].bitcast(I32))
+        nc.sync.dma_start(out=w2_codes[:].bitcast(I32), in_=w2_words[0].bitcast(I32))
+        load_scale_rows(nc.sync, w3_plane, w3_scales)
+        load_scale_rows(nc.sync, w2_plane, w2_scales)
+
+        ident = keep.tile([P, P], F32, name="ident")
+        make_identity(nc, ident[:])
+
+        picked_plane = keep.tile([P, S], U8, name="picked_plane", align_bytes=64)
+        nc.vector.tensor_copy(picked_plane[:], x_plane[:].indirect(offs_list[:]))
+        picked = []
+        for half in range(2):
+            words = keep.tile([P, BANK], U32, name="picked%d" % half, align_bytes=64)
+            cols = slice(half * BANK // LIST_ROWS, (half + 1) * BANK // LIST_ROWS)
+            nc.vector.tensor_copy(words[:], x_table[:].indirect(offs_list[:, cols]))
+            picked.append(words)
+
+        w1_bf = keep.tile([P, PACK, P, PACK], BF16, name="w1_bf", align_bytes=64)
+        for half in range(2):
+            dst = w1_bf[:, :, half * 64 : (half + 1) * 64, :].rearrange("p t m j -> p m t j")
+            src = w1_raw[half][:].rearrange("p j (m t) -> p m t j", t=PACK)
+            if half == 0:
+                nc.scalar.activation(dst, src, COPY)
+            else:
+                nc.vector.tensor_copy(dst, src)
+        w1_codes = keep.tile([P, H], U32, name="w1_codes", align_bytes=64)
+        w1_plane = keep.tile([P, H], U8, name="w1_plane", align_bytes=64)
+        for t in range(PACK):
+            cols = slice(t * P, (t + 1) * P)
+            nc.vector.quantize_mx(
+                out=w1_codes[:, cols].bitcast(FP8X4),
+                scales=w1_plane[:, cols],
+                in_=w1_bf[:, t].rearrange("p m j -> p (m j)"),
+            )
+
+        h = []
+        for t in range(PACK):
+            cols = slice(t * P, (t + 1) * P)
+            h_t = keep.tile([P, S], F32, name="h%d" % t)
+            for half in range(2):
+                part = slice(half * BANK, (half + 1) * BANK)
+                acc = psum.tile([P, BANK], F32, name="acc", tag="acc", bufs=4)
+                nc.tensor.matmul_mx(
+                    out=acc[:],
+                    lhsT=w1_codes[:, cols].bitcast(FP8X4),
+                    lhsT_scale=w1_plane[:, cols],
+                    rhs=picked[half][:].bitcast(FP8X4),
+                    rhs_scale=picked_plane[:, part],
+                    start=True,
+                    stop=True,
+                )
+                if t == 0 and half == 1:
+                    nc.vector.tensor_scalar_max(h_t[:, part], acc[:], 0.0)
+                else:
+                    nc.scalar.activation(h_t[:, part], acc[:], RELU)
+            h.append(h_t)
+
+        z_words = []
+        for u in range(2):
+            sums = [psum.tile([P, 2, P], F32, name="sums%d" % b, tag="sums%d" % b) for b in range(BLOCKS)]
+            for e in range(2):
+                t = 2 * u + e
+                for d in range(3):
+                    got = keep.tile([P, V], F32, name="got", tag="got%d_%d" % (t, d))
+                    nc.vector.tensor_copy(got[:], h[t][:].indirect(pos_lists[d][:]))
+                    for b in range(BLOCKS):
+                        nc.tensor.matmul(
+                            sums[b][:, e, :],
+                            got[:, b * P : (b + 1) * P],
+                            ident[:],
+                            start=(d == 0),
+                            stop=(d == 2),
+                            is_transpose=True,
+                        )
+            pairs = []
+            for b in range(BLOCKS):
+                pair = keep.tile([P, 2 * P], BF16, name="pair", tag="pair%d_%d" % (u, b), align_bytes=64)
+                nc.scalar.activation(
+                    pair[:].rearrange("v (p e) -> v p e", e=2), sums[b][:].rearrange("v e p -> v p e"), COPY, scale=1.0 / 3.0
+                )
+                pairs.append(pair)
+            z_words.append(pairs)
+
+        z_bf = keep.tile([P, V * PACK], BF16, name="z_bf", align_bytes=64)
+        for b in range(BLOCKS):
+            back = psum.tile([P, 2, P], F32, name="back", tag="acc", bufs=4)
+            for u in range(2):
+                nc.tensor.transpose(back[:, u, :], z_words[u][b][:].bitcast(F32), ident[:])
+            nc.scalar.copy(
+                z_bf[:, b * BANK : (b + 1) * BANK].bitcast(F32).rearrange("p (v u) -> p v u", u=2),
+                back[:].rearrange("p u v -> p v u"),
+            )
+
+        hc_bf = []
+        for i, (a, b) in enumerate(CEN_PIECES):
+            n = b - a
+            planes = keep.tile([P, PACK, n], F32, name="planes", tag="got%d_%d" % (PACK - 1, i))
+            for t in range(PACK):
+                nc.vector.tensor_copy(planes[:, t, :], h[t][:].indirect(cen_list[:, a // LIST_ROWS : b // LIST_ROWS]))
+            tag = "pair1_%d" % (BLOCKS - 1) if i == 0 else "hc_bf%d" % i
+            piece = keep.tile([P, n, PACK], BF16, name="hc_bf", tag=tag, align_bytes=64)
+            nc.scalar.copy(piece[:], planes[:].rearrange("p t n -> p n t"))
+            hc_bf.append(piece)
+
+        z_codes = keep.tile([P, V], U32, name="z_codes", align_bytes=64)
+        z_plane = keep.tile([P, V], U8, name="z_plane", align_bytes=64)
+        nc.vector.quantize_mx(out=z_codes[:].bitcast(FP8X4), scales=z_plane[:], in_=z_bf[:])
+        for i, (a, b) in enumerate(CEN_PIECES):
+            n = b - a
+            hc_codes = keep.tile([P, n], U32, name="hc_codes%d" % i, align_bytes=64)
+            hc_plane = keep.tile([P, n], U8, name="hc_plane%d" % i, align_bytes=64)
+            nc.vector.quantize_mx(
+                out=hc_codes[:].bitcast(FP8X4), scales=hc_plane[:], in_=hc_bf[i][:].rearrange("p n t -> p (n t)")
+            )
+            result = keep.tile([P, n], F32, name="result%d" % i)
+            for c in range(0, n, P):
+                cols = slice(a + c, a + c + P)
+                total = psum.tile([P, P], F32, name="total", tag="sums%d" % ((a + c) // P))
+                nc.tensor.matmul_mx(
+                    out=total[:],
+                    lhsT=w3_codes[:].bitcast(FP4X4),
+                    lhsT_scale=w3_plane[:],
+                    rhs=z_codes[:, cols].bitcast(FP8X4),
+                    rhs_scale=z_plane[:, cols],
+                    start=True,
+                    stop=False,
+                )
+                nc.tensor.matmul_mx(
+                    out=total[:],
+                    lhsT=w2_codes[:].bitcast(FP4X4),
+                    lhsT_scale=w2_plane[:],
+                    rhs=hc_codes[:, c : c + P].bitcast(FP8X4),
+                    rhs_scale=hc_plane[:, c : c + P],
+                    start=False,
+                    stop=True,
+                )
+                nc.scalar.copy(result[:, c : c + P], total[:])
+            nc.sync.dma_start(out=out[:, a:b], in_=result[:])

@@ -51,16 +51,16 @@ def tile_picked_sagecat_mean_p_kernel(
         nc.vector.memset(w2_plane[:].bitcast(I32), 0)
         nc.vector.memset(w3_plane[:].bitcast(I32), 0)
 
+        ident = keep.tile([P, P], F32, name="ident")
+        nc.vector.memset(ident[:], 0.0)
+        make_identity(nc, ident[:], nomemset=True)
+
         offs_list = load_list("offs_list", offs)
+        w1_raw = keep.tile([P, PACK, H], F32, name="w1_raw")
+        nc.sync.dma_start(out=w1_raw[:], in_=w1.rearrange("(p j) c -> p j c", j=PACK))
+        load_scale_rows(nc.sync, x_plane, x_scales)
         x_table = keep.tile([P, T], U32, name="x_table")
         nc.sync.dma_start(out=x_table[:].bitcast(I32), in_=x_words[0].rearrange("p n t -> p (n t)").bitcast(I32))
-        load_scale_rows(nc.scalar, x_plane, x_scales)
-        w1_rows = w1.rearrange("(p j) c -> p j c", j=PACK)
-        w1_raw = []
-        for half in range(2):
-            raw = keep.tile([P, PACK, H // 2], F32, name="w1_raw%d" % half)
-            nc.sync.dma_start(out=raw[:], in_=w1_rows[:, :, half * (H // 2) : (half + 1) * (H // 2)])
-            w1_raw.append(raw)
         pos_lists = [load_list("pos%d_list" % d, src) for d, src in enumerate((pos1, pos2, pos3))]
         cen_list = load_list("cen_list", cen)
         w2_codes = keep.tile([P, 2 * N], U8, name="w2_codes", align_bytes=64)
@@ -70,22 +70,13 @@ def tile_picked_sagecat_mean_p_kernel(
         load_scale_rows(nc.sync, w3_plane, w3_scales)
         load_scale_rows(nc.sync, w2_plane, w2_scales)
 
-        ident = keep.tile([P, P], F32, name="ident")
-        make_identity(nc, ident[:])
-
         picked_plane = keep.tile([P, S], U8, name="picked_plane", align_bytes=64)
         nc.vector.tensor_copy(picked_plane[:], x_plane[:].indirect(offs_list[:]))
-        picked = []
-        for half in range(2):
-            words = keep.tile([P, BANK], U32, name="picked%d" % half, align_bytes=64)
-            cols = slice(half * BANK // LIST_ROWS, (half + 1) * BANK // LIST_ROWS)
-            nc.vector.tensor_copy(words[:], x_table[:].indirect(offs_list[:, cols]))
-            picked.append(words)
 
         w1_bf = keep.tile([P, PACK, P, PACK], BF16, name="w1_bf", align_bytes=64)
         for half in range(2):
             dst = w1_bf[:, :, half * 64 : (half + 1) * 64, :].rearrange("p t m j -> p m t j")
-            src = w1_raw[half][:].rearrange("p j (m t) -> p m t j", t=PACK)
+            src = w1_raw[:, :, half * (H // 2) : (half + 1) * (H // 2)].rearrange("p j (m t) -> p m t j", t=PACK)
             if half == 0:
                 nc.scalar.activation(dst, src, COPY)
             else:
@@ -100,78 +91,105 @@ def tile_picked_sagecat_mean_p_kernel(
                 in_=w1_bf[:, t].rearrange("p m j -> p (m j)"),
             )
 
+        picked = []
+        for half in range(2):
+            words = keep.tile([P, BANK], U32, name="picked%d" % half, align_bytes=64)
+            cols = slice(half * BANK // LIST_ROWS, (half + 1) * BANK // LIST_ROWS)
+            nc.vector.tensor_copy(words[:], x_table[:].indirect(offs_list[:, cols]))
+            picked.append(words)
+
         h = []
         for t in range(PACK):
             cols = slice(t * P, (t + 1) * P)
             h_t = keep.tile([P, S], F32, name="h%d" % t)
-            for half in range(2):
-                part = slice(half * BANK, (half + 1) * BANK)
-                acc = psum.tile([P, BANK], F32, name="acc", tag="acc", bufs=4)
+            parts = ((0, 512), (512, 768), (768, 1024)) if t == 0 else ((0, 512), (512, 1024))
+            for a, b in parts:
+                half = a // BANK
+                acc = psum.tile([P, b - a], F32, name="acc", tag="acc", bufs=4)
                 nc.tensor.matmul_mx(
                     out=acc[:],
                     lhsT=w1_codes[:, cols].bitcast(FP8X4),
                     lhsT_scale=w1_plane[:, cols],
-                    rhs=picked[half][:].bitcast(FP8X4),
-                    rhs_scale=picked_plane[:, part],
+                    rhs=picked[half][:, a - half * BANK : b - half * BANK].bitcast(FP8X4),
+                    rhs_scale=picked_plane[:, a:b],
                     start=True,
                     stop=True,
                 )
-                if t == 0 and half == 1:
-                    nc.vector.tensor_scalar_max(h_t[:, part], acc[:], 0.0)
+                if t == 0 and b == S:
+                    nc.vector.tensor_scalar_max(h_t[:, a:b], acc[:], 0.0)
                 else:
-                    nc.scalar.activation(h_t[:, part], acc[:], RELU)
+                    nc.scalar.activation(h_t[:, a:b], acc[:], RELU)
             h.append(h_t)
 
-        z_words = []
-        for u in range(2):
-            sums = [psum.tile([P, 2, P], F32, name="sums%d" % b, tag="sums%d" % b) for b in range(BLOCKS)]
-            for e in range(2):
-                t = 2 * u + e
-                for d in range(3):
-                    got = keep.tile([P, V], F32, name="got", tag="got%d_%d" % (t, d))
-                    nc.vector.tensor_copy(got[:], h[t][:].indirect(pos_lists[d][:]))
-                    for b in range(BLOCKS):
-                        nc.tensor.matmul(
-                            sums[b][:, e, :],
-                            got[:, b * P : (b + 1) * P],
-                            ident[:],
-                            start=(d == 0),
-                            stop=(d == 2),
-                            is_transpose=True,
-                        )
-            pairs = []
-            for b in range(BLOCKS):
-                pair = keep.tile([P, 2 * P], BF16, name="pair", tag="pair%d_%d" % (u, b), align_bytes=64)
-                nc.scalar.activation(
-                    pair[:].rearrange("v (p e) -> v p e", e=2), sums[b][:].rearrange("v e p -> v p e"), COPY, scale=1.0 / 3.0
-                )
-                pairs.append(pair)
-            z_words.append(pairs)
+        def centres(i, planes_tag, piece_tag):
+            a, b = CEN_PIECES[i]
+            n = b - a
+            planes = keep.tile([P, PACK, n], F32, name="planes", tag=planes_tag)
+            for t in range(PACK):
+                nc.vector.tensor_copy(planes[:, t, :], h[t][:].indirect(cen_list[:, a // LIST_ROWS : b // LIST_ROWS]))
+            piece = keep.tile([P, n, PACK], BF16, name="hc_bf", tag=piece_tag, align_bytes=64)
+            nc.scalar.copy(
+                piece[:].rearrange("p (c i) t -> p c t i", i=4), planes[:].rearrange("p t (c i) -> p c t i", i=4)
+            )
+            return piece
 
-        z_bf = keep.tile([P, V * PACK], BF16, name="z_bf", align_bytes=64)
-        for b in range(BLOCKS):
+        def neighbours(t, a, b, sums):
+            for d in range(3):
+                got = keep.tile([P, b - a], F32, name="got", tag=("odd%d" if t == 1 else "got%d") % d)
+                nc.vector.tensor_copy(got[:], h[t][:].indirect(pos_lists[d][:, a // LIST_ROWS : b // LIST_ROWS]))
+                for c in range(a, b, P):
+                    nc.tensor.matmul(
+                        sums[c // P][:, t % 2, :],
+                        got[:, c - a : c - a + P],
+                        ident[:],
+                        start=(d == 0),
+                        stop=(d == 2),
+                        is_transpose=True,
+                    )
+
+        def mean_pairs(u, b, sums):
+            pair = keep.tile([P, 2 * P], BF16, name="pair", tag="pair%d_%d" % (u, b), align_bytes=64)
+            nc.scalar.activation(
+                pair[:].rearrange("v (p e) -> v p e", e=2), sums[b][:].rearrange("v e p -> v p e"), COPY, scale=1.0 / 3.0
+            )
+            return pair
+
+        def turn_back(b, pairs, z_half):
             back = psum.tile([P, 2, P], F32, name="back", tag="acc", bufs=4)
             for u in range(2):
-                nc.tensor.transpose(back[:, u, :], z_words[u][b][:].bitcast(F32), ident[:])
+                nc.tensor.transpose(back[:, u, :], pairs[u][:].bitcast(F32), ident[:])
+            c = (b % 2) * P * PACK
             nc.scalar.copy(
-                z_bf[:, b * BANK : (b + 1) * BANK].bitcast(F32).rearrange("p (v u) -> p v u", u=2),
+                z_half[:, c : c + P * PACK].bitcast(F32).rearrange("p (v u) -> p v u", u=2),
                 back[:].rearrange("p u v -> p v u"),
             )
 
-        hc_bf = []
-        for i, (a, b) in enumerate(CEN_PIECES):
-            n = b - a
-            planes = keep.tile([P, PACK, n], F32, name="planes", tag="got%d_%d" % (PACK - 1, i))
-            for t in range(PACK):
-                nc.vector.tensor_copy(planes[:, t, :], h[t][:].indirect(cen_list[:, a // LIST_ROWS : b // LIST_ROWS]))
-            tag = "pair1_%d" % (BLOCKS - 1) if i == 0 else "hc_bf%d" % i
-            piece = keep.tile([P, n, PACK], BF16, name="hc_bf", tag=tag, align_bytes=64)
-            nc.scalar.copy(piece[:], planes[:].rearrange("p t n -> p n t"))
-            hc_bf.append(piece)
+        sums = [psum.tile([P, 2, P], F32, name="sums", tag="sums%d" % b) for b in range(BLOCKS)]
+        neighbours(0, 0, V, sums)
+        neighbours(1, 0, V, sums)
+        low_pairs = [mean_pairs(0, b, sums) for b in range(BLOCKS)]
+        sums = [psum.tile([P, 2, P], F32, name="sums", tag="sums%d" % b) for b in range(BLOCKS)]
+        neighbours(2, 0, V, sums)
+        hc_bf = [centres(0, "odd2", "hc_bf0")]
+        z_bf = []
+        for half in range(2):
+            neighbours(3, half * V // 2, (half + 1) * V // 2, sums)
+            z_half = keep.tile([P, V // 2 * PACK], BF16, name="z_bf%d" % half, align_bytes=64)
+            blocks = (2 * half, 2 * half + 1)
+            high_pairs = [mean_pairs(1, b, sums) for b in blocks]
+            for b, high in zip(blocks, high_pairs):
+                turn_back(b, (low_pairs[b], high), z_half)
+            z_bf.append(z_half)
+        hc_bf.append(centres(1, "got0", "pair1_3"))
+        hc_bf.append(centres(2, "got1", "hc_bf2"))
 
-        z_codes = keep.tile([P, V], U32, name="z_codes", align_bytes=64)
-        z_plane = keep.tile([P, V], U8, name="z_plane", align_bytes=64)
-        nc.vector.quantize_mx(out=z_codes[:].bitcast(FP8X4), scales=z_plane[:], in_=z_bf[:])
+        z_codes, z_plane = [], []
+        for half in range(2):
+            codes = keep.tile([P, V // 2], U32, name="z_codes%d" % half, align_bytes=64)
+            plane = keep.tile([P, V // 2], U8, name="z_plane%d" % half, align_bytes=64)
+            nc.vector.quantize_mx(out=codes[:].bitcast(FP8X4), scales=plane[:], in_=z_bf[half][:])
+            z_codes.append(codes)
+            z_plane.append(plane)
         for i, (a, b) in enumerate(CEN_PIECES):
             n = b - a
             hc_codes = keep.tile([P, n], U32, name="hc_codes%d" % i, align_bytes=64)
@@ -181,14 +199,15 @@ def tile_picked_sagecat_mean_p_kernel(
             )
             result = keep.tile([P, n], F32, name="result%d" % i)
             for c in range(0, n, P):
-                cols = slice(a + c, a + c + P)
+                half, c0 = divmod(a + c, V // 2)
+                cols = slice(c0, c0 + P)
                 total = psum.tile([P, P], F32, name="total", tag="sums%d" % ((a + c) // P))
                 nc.tensor.matmul_mx(
                     out=total[:],
                     lhsT=w3_codes[:].bitcast(FP4X4),
                     lhsT_scale=w3_plane[:],
-                    rhs=z_codes[:, cols].bitcast(FP8X4),
-                    rhs_scale=z_plane[:, cols],
+                    rhs=z_codes[half][:, cols].bitcast(FP8X4),
+                    rhs_scale=z_plane[half][:, cols],
                     start=True,
                     stop=False,
                 )

@@ -38,14 +38,14 @@ def tile_picked_sagecat_mean_p_kernel(
             nc.sync.dma_start(tile[:], src)
             return tile
 
-        def load_scale_rows(queue, plane, rows):
-            for q in range(4):
-                queue.dma_start(
-                    out=plane[32 * q : 32 * q + 4, :].bitcast(I32), in_=rows[0, 4 * q : 4 * q + 4, :].bitcast(I32)
-                )
+        def place_scale_rows(queue, plane, rows):
+            for r in range(4):
+                queue.dma_start(out=plane[r:P:32, :].bitcast(I32), in_=rows(r).bitcast(I32))
 
         x_plane = keep.tile([P, T], U8, name="x_plane")
         nc.vector.memset(x_plane[:].bitcast(I32), 0)
+        picked_plane = keep.tile([P, S], U8, name="picked_plane", align_bytes=64)
+        nc.vector.memset(picked_plane[:].bitcast(I32), 0)
         w2_plane = keep.tile([P, N], U8, name="w2_plane", align_bytes=64)
         w3_plane = keep.tile([P, N], U8, name="w3_plane", align_bytes=64)
         nc.vector.memset(w2_plane[:].bitcast(I32), 0)
@@ -58,29 +58,27 @@ def tile_picked_sagecat_mean_p_kernel(
         offs_list = load_list("offs_list", offs)
         w1_raw = keep.tile([P, PACK, H], F32, name="w1_raw")
         nc.sync.dma_start(out=w1_raw[:], in_=w1.rearrange("(p j) c -> p j c", j=PACK))
-        load_scale_rows(nc.sync, x_plane, x_scales)
+        nc.sync.dma_start(out=x_plane[0:P:8, :].bitcast(I32), in_=x_scales[0].bitcast(I32))
         x_table = keep.tile([P, T], U32, name="x_table")
         nc.sync.dma_start(out=x_table[:].bitcast(I32), in_=x_words[0].rearrange("p n t -> p (n t)").bitcast(I32))
+        picked_rows = keep.tile([P, S], U8, name="picked_rows")
+        nc.vector.tensor_copy(picked_rows[:], x_plane[:].indirect(offs_list[:]))
+        place_scale_rows(nc.sync, picked_plane, lambda r: picked_rows[8 * r : P : 32, :])
+
         pos_lists = [load_list("pos%d_list" % d, src) for d, src in enumerate((pos1, pos2, pos3))]
         cen_list = load_list("cen_list", cen)
         w2_codes = keep.tile([P, 2 * N], U8, name="w2_codes", align_bytes=64)
         w3_codes = keep.tile([P, 2 * N], U8, name="w3_codes", align_bytes=64)
         nc.sync.dma_start(out=w3_codes[:].bitcast(I32), in_=w3_words[0].bitcast(I32))
         nc.sync.dma_start(out=w2_codes[:].bitcast(I32), in_=w2_words[0].bitcast(I32))
-        load_scale_rows(nc.sync, w3_plane, w3_scales)
-        load_scale_rows(nc.sync, w2_plane, w2_scales)
-
-        picked_plane = keep.tile([P, S], U8, name="picked_plane", align_bytes=64)
-        nc.vector.tensor_copy(picked_plane[:], x_plane[:].indirect(offs_list[:]))
+        place_scale_rows(nc.sync, w3_plane, lambda r: w3_scales[0, r:16:4, :])
+        place_scale_rows(nc.sync, w2_plane, lambda r: w2_scales[0, r:16:4, :])
 
         w1_bf = keep.tile([P, PACK, P, PACK], BF16, name="w1_bf", align_bytes=64)
-        for half in range(2):
-            dst = w1_bf[:, :, half * 64 : (half + 1) * 64, :].rearrange("p t m j -> p m t j")
-            src = w1_raw[:, :, half * (H // 2) : (half + 1) * (H // 2)].rearrange("p j (m t) -> p m t j", t=PACK)
-            if half == 0:
-                nc.scalar.activation(dst, src, COPY)
-            else:
-                nc.vector.tensor_copy(dst, src)
+        dealt = w1_bf[:].rearrange("p t m j -> p m t j")
+        rows = w1_raw[:].rearrange("p j (m t) -> p m t j", t=PACK)
+        nc.scalar.copy(dealt[:, :96], rows[:, :96])
+        nc.vector.tensor_copy(dealt[:, 96:], rows[:, 96:])
         w1_codes = keep.tile([P, H], U32, name="w1_codes", align_bytes=64)
         w1_plane = keep.tile([P, H], U8, name="w1_plane", align_bytes=64)
         for t in range(PACK):
@@ -115,7 +113,7 @@ def tile_picked_sagecat_mean_p_kernel(
                     start=True,
                     stop=True,
                 )
-                if t == 0 and b == S:
+                if t == 0 and b == 768:
                     nc.vector.tensor_scalar_max(h_t[:, a:b], acc[:], 0.0)
                 else:
                     nc.scalar.activation(h_t[:, a:b], acc[:], RELU)
@@ -124,7 +122,7 @@ def tile_picked_sagecat_mean_p_kernel(
         def centres(i, planes_tag, piece_tag):
             a, b = CEN_PIECES[i]
             n = b - a
-            planes = keep.tile([P, PACK, n], F32, name="planes", tag=planes_tag)
+            planes = keep.tile([P, PACK, n], F32, name="planes", tag=planes_tag, align_bytes=64)
             for t in range(PACK):
                 nc.vector.tensor_copy(planes[:, t, :], h[t][:].indirect(cen_list[:, a // LIST_ROWS : b // LIST_ROWS]))
             piece = keep.tile([P, n, PACK], BF16, name="hc_bf", tag=piece_tag, align_bytes=64)
@@ -133,9 +131,9 @@ def tile_picked_sagecat_mean_p_kernel(
             )
             return piece
 
-        def neighbours(t, a, b, sums):
+        def neighbours(t, a, b, sums, tags):
             for d in range(3):
-                got = keep.tile([P, b - a], F32, name="got", tag=("odd%d" if t == 1 else "got%d") % d)
+                got = keep.tile([P, b - a], F32, name="got", tag=tags[d], align_bytes=64)
                 nc.vector.tensor_copy(got[:], h[t][:].indirect(pos_lists[d][:, a // LIST_ROWS : b // LIST_ROWS]))
                 for c in range(a, b, P):
                     nc.tensor.matmul(
@@ -164,24 +162,27 @@ def tile_picked_sagecat_mean_p_kernel(
                 back[:].rearrange("p u v -> p v u"),
             )
 
-        sums = [psum.tile([P, 2, P], F32, name="sums", tag="sums%d" % b) for b in range(BLOCKS)]
-        neighbours(0, 0, V, sums)
-        neighbours(1, 0, V, sums)
-        low_pairs = [mean_pairs(0, b, sums) for b in range(BLOCKS)]
-        sums = [psum.tile([P, 2, P], F32, name="sums", tag="sums%d" % b) for b in range(BLOCKS)]
-        neighbours(2, 0, V, sums)
-        hc_bf = [centres(0, "odd2", "hc_bf0")]
-        z_bf = []
-        for half in range(2):
-            neighbours(3, half * V // 2, (half + 1) * V // 2, sums)
+        def finish_means(half, sums, low_pairs):
             z_half = keep.tile([P, V // 2 * PACK], BF16, name="z_bf%d" % half, align_bytes=64)
             blocks = (2 * half, 2 * half + 1)
             high_pairs = [mean_pairs(1, b, sums) for b in blocks]
             for b, high in zip(blocks, high_pairs):
                 turn_back(b, (low_pairs[b], high), z_half)
-            z_bf.append(z_half)
-        hc_bf.append(centres(1, "got0", "pair1_3"))
-        hc_bf.append(centres(2, "got1", "hc_bf2"))
+            return z_half
+
+        even = ("even0", "even1", "even2")
+        odd = ("odd0", "odd1", "odd2")
+        sums = [psum.tile([P, 2, P], F32, name="sums", tag="sums%d" % b) for b in range(BLOCKS)]
+        neighbours(0, 0, V, sums, even)
+        neighbours(1, 0, V, sums, odd)
+        low_pairs = [mean_pairs(0, b, sums) for b in range(BLOCKS)]
+        sums = [psum.tile([P, 2, P], F32, name="sums", tag="sums%d" % b) for b in range(BLOCKS)]
+        neighbours(2, 0, V, sums, even)
+        neighbours(3, 0, V // 2, sums, even)
+        z_bf = [finish_means(0, sums, low_pairs)]
+        neighbours(3, V // 2, V, sums, ("even0", "even1", "pair0_0"))
+        z_bf.append(finish_means(1, sums, low_pairs))
+        hc_bf = [centres(0, "even0", "pair1_3"), centres(1, "even1", "hc_bf1"), centres(2, "pair0_0", "hc_bf2")]
 
         z_codes, z_plane = [], []
         for half in range(2):
@@ -197,7 +198,7 @@ def tile_picked_sagecat_mean_p_kernel(
             nc.vector.quantize_mx(
                 out=hc_codes[:].bitcast(FP8X4), scales=hc_plane[:], in_=hc_bf[i][:].rearrange("p n t -> p (n t)")
             )
-            result = keep.tile([P, n], F32, name="result%d" % i)
+            result = keep.tile([P, n], F32, name="result", tag="pair0_0" if i == 0 else "result%d" % i, align_bytes=64)
             for c in range(0, n, P):
                 half, c0 = divmod(a + c, V // 2)
                 cols = slice(c0, c0 + P)
@@ -220,5 +221,8 @@ def tile_picked_sagecat_mean_p_kernel(
                     start=False,
                     stop=True,
                 )
-                nc.scalar.copy(result[:, c : c + P], total[:])
+                if b == V:
+                    nc.vector.tensor_copy(result[:, c : c + P], total[:])
+                else:
+                    nc.scalar.copy(result[:, c : c + P], total[:])
             nc.sync.dma_start(out=out[:, a:b], in_=result[:])

@@ -22,6 +22,10 @@ PACK = 4
 BANK = 512
 LIST_ROWS = 16
 BLOCKS = V // P
+X_FIRST = 1024
+FIRST_ON_SCALAR = 40
+FIRST_PARTS = ((0, 256), (256, 512), (512, 768), (768, 896), (896, 1024))
+CAST_TAGS = ("w1_bf0", "w1_bf1", "w1_bf0", "w1_codes0")
 CEN_PIECES = ((0, 256), (256, 384), (384, 512))
 
 
@@ -55,15 +59,17 @@ def tile_picked_sagecat_mean_p_kernel(
         nc.vector.memset(ident[:], 0.0)
         make_identity(nc, ident[:], nomemset=True)
 
+        x_table = keep.tile([P, T], U32, name="x_table")
+        x_src = x_words[0].rearrange("p n t -> p (n t)").bitcast(I32)
+        nc.sync.dma_start(out=x_table[:, :X_FIRST].bitcast(I32), in_=x_src[:, :X_FIRST])
         offs_list = load_list("offs_list", offs)
+        nc.sync.dma_start(out=x_plane[0:P:8, :].bitcast(I32), in_=x_scales[0].bitcast(I32))
+        nc.sync.dma_start(out=x_table[:, X_FIRST:].bitcast(I32), in_=x_src[:, X_FIRST:])
         w1_raw = keep.tile([P, PACK, H], F32, name="w1_raw")
         nc.sync.dma_start(out=w1_raw[:], in_=w1.rearrange("(p j) c -> p j c", j=PACK))
-        nc.sync.dma_start(out=x_plane[0:P:8, :].bitcast(I32), in_=x_scales[0].bitcast(I32))
-        x_table = keep.tile([P, T], U32, name="x_table")
-        nc.sync.dma_start(out=x_table[:].bitcast(I32), in_=x_words[0].rearrange("p n t -> p (n t)").bitcast(I32))
         picked_rows = keep.tile([P, S], U8, name="picked_rows")
         nc.vector.tensor_copy(picked_rows[:], x_plane[:].indirect(offs_list[:]))
-        place_scale_rows(nc.sync, picked_plane, lambda r: picked_rows[8 * r : P : 32, :])
+        place_scale_rows(nc.scalar, picked_plane, lambda r: picked_rows[8 * r : P : 32, :])
 
         pos_lists = [load_list("pos%d_list" % d, src) for d, src in enumerate((pos1, pos2, pos3))]
         cen_list = load_list("cen_list", cen)
@@ -74,21 +80,6 @@ def tile_picked_sagecat_mean_p_kernel(
         place_scale_rows(nc.sync, w3_plane, lambda r: w3_scales[0, r:16:4, :])
         place_scale_rows(nc.sync, w2_plane, lambda r: w2_scales[0, r:16:4, :])
 
-        w1_bf = keep.tile([P, PACK, P, PACK], BF16, name="w1_bf", align_bytes=64)
-        dealt = w1_bf[:].rearrange("p t m j -> p m t j")
-        rows = w1_raw[:].rearrange("p j (m t) -> p m t j", t=PACK)
-        nc.scalar.copy(dealt[:, :96], rows[:, :96])
-        nc.vector.tensor_copy(dealt[:, 96:], rows[:, 96:])
-        w1_codes = keep.tile([P, H], U32, name="w1_codes", align_bytes=64)
-        w1_plane = keep.tile([P, H], U8, name="w1_plane", align_bytes=64)
-        for t in range(PACK):
-            cols = slice(t * P, (t + 1) * P)
-            nc.vector.quantize_mx(
-                out=w1_codes[:, cols].bitcast(FP8X4),
-                scales=w1_plane[:, cols],
-                in_=w1_bf[:, t].rearrange("p m j -> p (m j)"),
-            )
-
         picked = []
         for half in range(2):
             words = keep.tile([P, BANK], U32, name="picked%d" % half, align_bytes=64)
@@ -96,28 +87,54 @@ def tile_picked_sagecat_mean_p_kernel(
             nc.vector.tensor_copy(words[:], x_table[:].indirect(offs_list[:, cols]))
             picked.append(words)
 
-        h = []
-        for t in range(PACK):
-            cols = slice(t * P, (t + 1) * P)
+        rows = w1_raw[:].rearrange("p j (m t) -> p t m j", t=PACK)
+
+        def cast_w1(t):
+            w1_bf = keep.tile([P, P, PACK], BF16, name="w1_bf", tag=CAST_TAGS[t], align_bytes=64)
+            if t == 0:
+                nc.scalar.copy(w1_bf[:, :FIRST_ON_SCALAR], rows[:, t, :FIRST_ON_SCALAR])
+                nc.vector.tensor_copy(w1_bf[:, FIRST_ON_SCALAR:], rows[:, t, FIRST_ON_SCALAR:])
+            elif t == 2:
+                nc.vector.tensor_copy(w1_bf[:], rows[:, t])
+            else:
+                nc.scalar.copy(w1_bf[:], rows[:, t])
+            return w1_bf
+
+        def quantise_w1(t, w1_bf):
+            codes = keep.tile([P, P], U32, name="w1_codes", tag="w1_codes%d" % t, align_bytes=64)
+            plane = keep.tile([P, P], U8, name="w1_plane%d" % t, align_bytes=64)
+            nc.vector.quantize_mx(
+                out=codes[:].bitcast(FP8X4), scales=plane[:], in_=w1_bf[:].rearrange("p m j -> p (m j)")
+            )
+            return codes, plane
+
+        def hidden(t, codes, plane):
             h_t = keep.tile([P, S], F32, name="h%d" % t)
-            parts = ((0, 512), (512, 768), (768, 1024)) if t == 0 else ((0, 512), (512, 1024))
-            for a, b in parts:
+            parts = FIRST_PARTS if t == 0 else ((0, 512), (512, 1024))
+            for i, (a, b) in enumerate(parts):
                 half = a // BANK
-                acc = psum.tile([P, b - a], F32, name="acc", tag="acc", bufs=4)
+                if t == 0 and i > 0:
+                    acc = psum.tile([P, b - a], F32, name="acc", tag="sums%d" % (i - 1))
+                else:
+                    acc = psum.tile([P, b - a], F32, name="acc", tag="acc", bufs=4)
                 nc.tensor.matmul_mx(
                     out=acc[:],
-                    lhsT=w1_codes[:, cols].bitcast(FP8X4),
-                    lhsT_scale=w1_plane[:, cols],
+                    lhsT=codes[:].bitcast(FP8X4),
+                    lhsT_scale=plane[:],
                     rhs=picked[half][:, a - half * BANK : b - half * BANK].bitcast(FP8X4),
                     rhs_scale=picked_plane[:, a:b],
                     start=True,
                     stop=True,
                 )
-                if t == 0 and b == 768:
+                if t == 0 and a in (512, 896):
                     nc.vector.tensor_scalar_max(h_t[:, a:b], acc[:], 0.0)
                 else:
                     nc.scalar.activation(h_t[:, a:b], acc[:], RELU)
-            h.append(h_t)
+            return h_t
+
+        h = []
+        for t in range(PACK):
+            h.append(hidden(t, *quantise_w1(t, cast_w1(t))))
 
         def centres(i, planes_tag, piece_tag):
             a, b = CEN_PIECES[i]
@@ -184,13 +201,23 @@ def tile_picked_sagecat_mean_p_kernel(
         z_bf.append(finish_means(1, sums, low_pairs))
         hc_bf = [centres(0, "even0", "pair1_3"), centres(1, "even1", "hc_bf1"), centres(2, "pair0_0", "hc_bf2")]
 
-        z_codes, z_plane = [], []
+        totals = []
         for half in range(2):
             codes = keep.tile([P, V // 2], U32, name="z_codes%d" % half, align_bytes=64)
             plane = keep.tile([P, V // 2], U8, name="z_plane%d" % half, align_bytes=64)
             nc.vector.quantize_mx(out=codes[:].bitcast(FP8X4), scales=plane[:], in_=z_bf[half][:])
-            z_codes.append(codes)
-            z_plane.append(plane)
+            for c in range(0, V // 2, P):
+                total = psum.tile([P, P], F32, name="total", tag="sums%d" % len(totals))
+                nc.tensor.matmul_mx(
+                    out=total[:],
+                    lhsT=w3_codes[:].bitcast(FP4X4),
+                    lhsT_scale=w3_plane[:],
+                    rhs=codes[:, c : c + P].bitcast(FP8X4),
+                    rhs_scale=plane[:, c : c + P],
+                    start=True,
+                    stop=False,
+                )
+                totals.append(total)
         for i, (a, b) in enumerate(CEN_PIECES):
             n = b - a
             hc_codes = keep.tile([P, n], U32, name="hc_codes%d" % i, align_bytes=64)
@@ -200,18 +227,7 @@ def tile_picked_sagecat_mean_p_kernel(
             )
             result = keep.tile([P, n], F32, name="result", tag="pair0_0" if i == 0 else "result%d" % i, align_bytes=64)
             for c in range(0, n, P):
-                half, c0 = divmod(a + c, V // 2)
-                cols = slice(c0, c0 + P)
-                total = psum.tile([P, P], F32, name="total", tag="sums%d" % ((a + c) // P))
-                nc.tensor.matmul_mx(
-                    out=total[:],
-                    lhsT=w3_codes[:].bitcast(FP4X4),
-                    lhsT_scale=w3_plane[:],
-                    rhs=z_codes[half][:, cols].bitcast(FP8X4),
-                    rhs_scale=z_plane[half][:, cols],
-                    start=True,
-                    stop=False,
-                )
+                total = totals[(a + c) // P]
                 nc.tensor.matmul_mx(
                     out=total[:],
                     lhsT=w2_codes[:].bitcast(FP4X4),

@@ -195,15 +195,15 @@ def tile_picked_sagecat_mean_p_kernel(
         low_pairs = [mean_pairs(0, b, sums) for b in range(BLOCKS)]
         sums = [psum.tile([P, 2, P], F32, name="sums", tag="sums%d" % b) for b in range(BLOCKS)]
         neighbours(2, 0, V, sums, even)
-        neighbours(3, 0, V // 2, sums, even)
+        neighbours(3, 0, V // 2, sums, odd)
         z_bf = [finish_means(0, sums, low_pairs)]
-        neighbours(3, V // 2, V, sums, ("even0", "even1", "pair0_0"))
+        neighbours(3, V // 2, V, sums, even)
         z_bf.append(finish_means(1, sums, low_pairs))
-        hc_bf = [centres(0, "even0", "pair1_3"), centres(1, "even1", "hc_bf1"), centres(2, "pair0_0", "hc_bf2")]
+        hc_bf = [centres(0, "odd0", "pair1_3"), centres(1, "odd1", "odd0"), centres(2, "odd2", "odd1")]
 
         totals = []
         for half in range(2):
-            codes = keep.tile([P, V // 2], U32, name="z_codes%d" % half, align_bytes=64)
+            codes = keep.tile([P, V // 2], U32, name="z_codes", tag=("pair0_3", "z_codes1")[half], align_bytes=64)
             plane = keep.tile([P, V // 2], U8, name="z_plane%d" % half, align_bytes=64)
             nc.vector.quantize_mx(out=codes[:].bitcast(FP8X4), scales=plane[:], in_=z_bf[half][:])
             for c in range(0, V // 2, P):
@@ -225,7 +225,7 @@ def tile_picked_sagecat_mean_p_kernel(
             nc.vector.quantize_mx(
                 out=hc_codes[:].bitcast(FP8X4), scales=hc_plane[:], in_=hc_bf[i][:].rearrange("p n t -> p (n t)")
             )
-            result = keep.tile([P, n], F32, name="result", tag="pair0_0" if i == 0 else "result%d" % i, align_bytes=64)
+            result = keep.tile([P, n], F32, name="result", tag="odd2" if i == 0 else "result%d" % i, align_bytes=64)
             for c in range(0, n, P):
                 total = totals[(a + c) // P]
                 nc.tensor.matmul_mx(

@@ -63,13 +63,13 @@ def tile_picked_sagecat_mean_p_kernel(
         x_src = x_words[0].rearrange("p n t -> p (n t)").bitcast(I32)
         nc.sync.dma_start(out=x_table[:, :X_FIRST].bitcast(I32), in_=x_src[:, :X_FIRST])
         offs_list = load_list("offs_list", offs)
-        nc.sync.dma_start(out=x_plane[0:P:8, :].bitcast(I32), in_=x_scales[0].bitcast(I32))
+        nc.sync.dma_start(out=x_plane[4:P:8, :].bitcast(I32), in_=x_scales[0].bitcast(I32))
         nc.sync.dma_start(out=x_table[:, X_FIRST:].bitcast(I32), in_=x_src[:, X_FIRST:])
         w1_raw = keep.tile([P, PACK, H], F32, name="w1_raw")
         nc.sync.dma_start(out=w1_raw[:], in_=w1.rearrange("(p j) c -> p j c", j=PACK))
         picked_rows = keep.tile([P, S], U8, name="picked_rows")
         nc.vector.tensor_copy(picked_rows[:], x_plane[:].indirect(offs_list[:]))
-        place_scale_rows(nc.scalar, picked_plane, lambda r: picked_rows[8 * r : P : 32, :])
+        place_scale_rows(nc.scalar, picked_plane, lambda r: picked_rows[4 + 8 * r : P : 32, :])
 
         pos_lists = [load_list("pos%d_list" % d, src) for d, src in enumerate((pos1, pos2, pos3))]
         cen_list = load_list("cen_list", cen)
@@ -171,7 +171,7 @@ def tile_picked_sagecat_mean_p_kernel(
 
         def turn_back(b, pairs, z_half):
             back = psum.tile([P, 2, P], F32, name="back", tag="acc", bufs=4)
-            for u in range(2):
+            for u in (1, 0):
                 nc.tensor.transpose(back[:, u, :], pairs[u][:].bitcast(F32), ident[:])
             c = (b % 2) * P * PACK
             nc.scalar.copy(
@@ -179,13 +179,10 @@ def tile_picked_sagecat_mean_p_kernel(
                 back[:].rearrange("p u v -> p v u"),
             )
 
-        def finish_means(half, sums, low_pairs):
-            z_half = keep.tile([P, V // 2 * PACK], BF16, name="z_bf%d" % half, align_bytes=64)
-            blocks = (2 * half, 2 * half + 1)
+        def finish_means(blocks, sums, low_pairs, z_bf):
             high_pairs = [mean_pairs(1, b, sums) for b in blocks]
             for b, high in zip(blocks, high_pairs):
-                turn_back(b, (low_pairs[b], high), z_half)
-            return z_half
+                turn_back(b, (low_pairs[b], high), z_bf[b // 2])
 
         even = ("even0", "even1", "even2")
         odd = ("odd0", "odd1", "odd2")
@@ -195,19 +192,20 @@ def tile_picked_sagecat_mean_p_kernel(
         low_pairs = [mean_pairs(0, b, sums) for b in range(BLOCKS)]
         sums = [psum.tile([P, 2, P], F32, name="sums", tag="sums%d" % b) for b in range(BLOCKS)]
         neighbours(2, 0, V, sums, even)
-        neighbours(3, 0, V // 2, sums, odd)
-        z_bf = [finish_means(0, sums, low_pairs)]
-        neighbours(3, V // 2, V, sums, even)
-        z_bf.append(finish_means(1, sums, low_pairs))
-        hc_bf = [centres(0, "odd0", "pair1_3"), centres(1, "odd1", "odd0"), centres(2, "odd2", "odd1")]
+        z_bf = [keep.tile([P, V // 2 * PACK], BF16, name="z_bf%d" % half, align_bytes=64) for half in range(2)]
+        neighbours(3, 0, V - P, sums, odd)
+        finish_means(range(BLOCKS - 1), sums, low_pairs, z_bf)
+        neighbours(3, V - P, V, sums, even)
+        finish_means(range(BLOCKS - 1, BLOCKS), sums, low_pairs, z_bf)
+        hc_bf = [centres(0, "odd0", "pair0_3"), centres(1, "odd1", "odd0"), centres(2, "odd2", "odd1")]
 
-        totals = []
-        for half in range(2):
-            codes = keep.tile([P, V // 2], U32, name="z_codes", tag=("pair0_3", "z_codes1")[half], align_bytes=64)
+        def neighbour_passes(half):
+            codes = keep.tile([P, V // 2], U32, name="z_codes", tag=("pair1_3", "z_codes1")[half], align_bytes=64)
             plane = keep.tile([P, V // 2], U8, name="z_plane%d" % half, align_bytes=64)
             nc.vector.quantize_mx(out=codes[:].bitcast(FP8X4), scales=plane[:], in_=z_bf[half][:])
+            totals = []
             for c in range(0, V // 2, P):
-                total = psum.tile([P, P], F32, name="total", tag="sums%d" % len(totals))
+                total = psum.tile([P, P], F32, name="total", tag="sums%d" % (2 * half + c // P))
                 nc.tensor.matmul_mx(
                     out=total[:],
                     lhsT=w3_codes[:].bitcast(FP4X4),
@@ -218,16 +216,17 @@ def tile_picked_sagecat_mean_p_kernel(
                     stop=False,
                 )
                 totals.append(total)
-        for i, (a, b) in enumerate(CEN_PIECES):
+            return totals
+
+        def centre_passes(i, totals):
+            a, b = CEN_PIECES[i]
             n = b - a
             hc_codes = keep.tile([P, n], U32, name="hc_codes%d" % i, align_bytes=64)
             hc_plane = keep.tile([P, n], U8, name="hc_plane%d" % i, align_bytes=64)
             nc.vector.quantize_mx(
                 out=hc_codes[:].bitcast(FP8X4), scales=hc_plane[:], in_=hc_bf[i][:].rearrange("p n t -> p (n t)")
             )
-            result = keep.tile([P, n], F32, name="result", tag="odd2" if i == 0 else "result%d" % i, align_bytes=64)
-            for c in range(0, n, P):
-                total = totals[(a + c) // P]
+            for c, total in zip(range(0, n, P), totals):
                 nc.tensor.matmul_mx(
                     out=total[:],
                     lhsT=w2_codes[:].bitcast(FP4X4),
@@ -237,8 +236,16 @@ def tile_picked_sagecat_mean_p_kernel(
                     start=False,
                     stop=True,
                 )
-                if b == V:
-                    nc.vector.tensor_copy(result[:, c : c + P], total[:])
+
+        totals = neighbour_passes(0) + neighbour_passes(1)
+        centre_passes(0, totals[:2])
+        centre_passes(1, totals[2:3])
+        centre_passes(2, totals[3:])
+        for i, (a, b) in enumerate(CEN_PIECES):
+            result = keep.tile([P, b - a], F32, name="result", tag="odd2" if i == 0 else "result%d" % i, align_bytes=64)
+            for c in range(a, b, P):
+                if c in (0, V - P):
+                    nc.vector.tensor_copy(result[:, c - a : c - a + P], totals[c // P][:])
                 else:
-                    nc.scalar.copy(result[:, c : c + P], total[:])
+                    nc.scalar.copy(result[:, c - a : c - a + P], totals[c // P][:])
             nc.sync.dma_start(out=out[:, a:b], in_=result[:])

@@ -21,10 +21,16 @@ P = 128
 PACK = 4
 BANK = 512
 LIST_ROWS = 16
+NEIGHBOURS = 3
 BLOCKS = V // P
+RING = 4
+ROW_STEP = P // 16
+ROW_FIRST = 4
 X_FIRST = 1024
 FIRST_ON_SCALAR = 40
 FIRST_PARTS = ((0, 256), (256, 512), (512, 768), (768, 896), (896, 1024))
+FIRST_ON_VECTOR = (2, 4)
+VECTOR_QUARTER = 2
 CAST_TAGS = ("w1_bf0", "w1_bf1", "w1_bf0", "w1_codes0")
 CEN_PIECES = ((0, 256), (256, 384), (384, 512))
 
@@ -42,12 +48,15 @@ def tile_picked_sagecat_mean_p_kernel(
             nc.sync.dma_start(tile[:], src)
             return tile
 
+        def entries(list_tile, a, b):
+            return list_tile[:, a // LIST_ROWS : b // LIST_ROWS]
+
         def place_scale_rows(queue, plane, rows):
             for r in range(4):
                 queue.dma_start(out=plane[r:P:32, :].bitcast(I32), in_=rows(r).bitcast(I32))
 
-        x_plane = keep.tile([P, T], U8, name="x_plane")
-        nc.vector.memset(x_plane[:].bitcast(I32), 0)
+        x_rows = keep.tile([P, T], U8, name="x_rows")
+        nc.vector.memset(x_rows[:].bitcast(I32), 0)
         picked_plane = keep.tile([P, S], U8, name="picked_plane", align_bytes=64)
         nc.vector.memset(picked_plane[:].bitcast(I32), 0)
         w2_plane = keep.tile([P, N], U8, name="w2_plane", align_bytes=64)
@@ -63,13 +72,14 @@ def tile_picked_sagecat_mean_p_kernel(
         x_src = x_words[0].rearrange("p n t -> p (n t)").bitcast(I32)
         nc.sync.dma_start(out=x_table[:, :X_FIRST].bitcast(I32), in_=x_src[:, :X_FIRST])
         offs_list = load_list("offs_list", offs)
-        nc.sync.dma_start(out=x_plane[4:P:8, :].bitcast(I32), in_=x_scales[0].bitcast(I32))
+        nc.sync.dma_start(out=x_rows[ROW_FIRST:P:ROW_STEP, :].bitcast(I32), in_=x_scales[0].bitcast(I32))
         nc.sync.dma_start(out=x_table[:, X_FIRST:].bitcast(I32), in_=x_src[:, X_FIRST:])
         w1_raw = keep.tile([P, PACK, H], F32, name="w1_raw")
         nc.sync.dma_start(out=w1_raw[:], in_=w1.rearrange("(p j) c -> p j c", j=PACK))
+
         picked_rows = keep.tile([P, S], U8, name="picked_rows")
-        nc.vector.tensor_copy(picked_rows[:], x_plane[:].indirect(offs_list[:]))
-        place_scale_rows(nc.scalar, picked_plane, lambda r: picked_rows[4 + 8 * r : P : 32, :])
+        nc.vector.tensor_copy(picked_rows[:], x_rows[:].indirect(offs_list[:]))
+        place_scale_rows(nc.sync, picked_plane, lambda r: picked_rows[ROW_FIRST + ROW_STEP * r : P : 32, :])
 
         pos_lists = [load_list("pos%d_list" % d, src) for d, src in enumerate((pos1, pos2, pos3))]
         cen_list = load_list("cen_list", cen)
@@ -81,23 +91,22 @@ def tile_picked_sagecat_mean_p_kernel(
         place_scale_rows(nc.sync, w2_plane, lambda r: w2_scales[0, r:16:4, :])
 
         picked = []
-        for half in range(2):
+        for half in range(S // BANK):
             words = keep.tile([P, BANK], U32, name="picked%d" % half, align_bytes=64)
-            cols = slice(half * BANK // LIST_ROWS, (half + 1) * BANK // LIST_ROWS)
-            nc.vector.tensor_copy(words[:], x_table[:].indirect(offs_list[:, cols]))
+            nc.vector.tensor_copy(words[:], x_table[:].indirect(entries(offs_list, half * BANK, (half + 1) * BANK)))
             picked.append(words)
 
-        rows = w1_raw[:].rearrange("p j (m t) -> p t m j", t=PACK)
+        dealt = w1_raw[:].rearrange("p j (m t) -> p t m j", t=PACK)
 
         def cast_w1(t):
             w1_bf = keep.tile([P, P, PACK], BF16, name="w1_bf", tag=CAST_TAGS[t], align_bytes=64)
             if t == 0:
-                nc.scalar.copy(w1_bf[:, :FIRST_ON_SCALAR], rows[:, t, :FIRST_ON_SCALAR])
-                nc.vector.tensor_copy(w1_bf[:, FIRST_ON_SCALAR:], rows[:, t, FIRST_ON_SCALAR:])
-            elif t == 2:
-                nc.vector.tensor_copy(w1_bf[:], rows[:, t])
+                nc.scalar.copy(w1_bf[:, :FIRST_ON_SCALAR], dealt[:, t, :FIRST_ON_SCALAR])
+                nc.vector.tensor_copy(w1_bf[:, FIRST_ON_SCALAR:], dealt[:, t, FIRST_ON_SCALAR:])
+            elif t == VECTOR_QUARTER:
+                nc.vector.tensor_copy(w1_bf[:], dealt[:, t])
             else:
-                nc.scalar.copy(w1_bf[:], rows[:, t])
+                nc.scalar.copy(w1_bf[:], dealt[:, t])
             return w1_bf
 
         def quantise_w1(t, w1_bf):
@@ -110,13 +119,13 @@ def tile_picked_sagecat_mean_p_kernel(
 
         def hidden(t, codes, plane):
             h_t = keep.tile([P, S], F32, name="h%d" % t)
-            parts = FIRST_PARTS if t == 0 else ((0, 512), (512, 1024))
-            for i, (a, b) in enumerate(parts):
+            parts = FIRST_PARTS if t == 0 else ((0, BANK), (BANK, S))
+            for part, (a, b) in enumerate(parts):
                 half = a // BANK
-                if t == 0 and i > 0:
-                    acc = psum.tile([P, b - a], F32, name="acc", tag="sums%d" % (i - 1))
+                if t == 0 and part > 0:
+                    acc = psum.tile([P, b - a], F32, name="acc", tag="block%d" % (part - 1))
                 else:
-                    acc = psum.tile([P, b - a], F32, name="acc", tag="acc", bufs=4)
+                    acc = psum.tile([P, b - a], F32, name="acc", tag="ring", bufs=RING)
                 nc.tensor.matmul_mx(
                     out=acc[:],
                     lhsT=codes[:].bitcast(FP8X4),
@@ -126,7 +135,7 @@ def tile_picked_sagecat_mean_p_kernel(
                     start=True,
                     stop=True,
                 )
-                if t == 0 and a in (512, 896):
+                if t == 0 and part in FIRST_ON_VECTOR:
                     nc.vector.tensor_scalar_max(h_t[:, a:b], acc[:], 0.0)
                 else:
                     nc.scalar.activation(h_t[:, a:b], acc[:], RELU)
@@ -136,76 +145,83 @@ def tile_picked_sagecat_mean_p_kernel(
         for t in range(PACK):
             h.append(hidden(t, *quantise_w1(t, cast_w1(t))))
 
-        def centres(i, planes_tag, piece_tag):
-            a, b = CEN_PIECES[i]
-            n = b - a
-            planes = keep.tile([P, PACK, n], F32, name="planes", tag=planes_tag, align_bytes=64)
-            for t in range(PACK):
-                nc.vector.tensor_copy(planes[:, t, :], h[t][:].indirect(cen_list[:, a // LIST_ROWS : b // LIST_ROWS]))
-            piece = keep.tile([P, n, PACK], BF16, name="hc_bf", tag=piece_tag, align_bytes=64)
-            nc.scalar.copy(
-                piece[:].rearrange("p (c i) t -> p c t i", i=4), planes[:].rearrange("p t (c i) -> p c t i", i=4)
-            )
-            return piece
-
         def neighbours(t, a, b, sums, tags):
-            for d in range(3):
+            for d in range(NEIGHBOURS):
                 got = keep.tile([P, b - a], F32, name="got", tag=tags[d], align_bytes=64)
-                nc.vector.tensor_copy(got[:], h[t][:].indirect(pos_lists[d][:, a // LIST_ROWS : b // LIST_ROWS]))
+                nc.vector.tensor_copy(got[:], h[t][:].indirect(entries(pos_lists[d], a, b)))
                 for c in range(a, b, P):
                     nc.tensor.matmul(
                         sums[c // P][:, t % 2, :],
                         got[:, c - a : c - a + P],
                         ident[:],
                         start=(d == 0),
-                        stop=(d == 2),
+                        stop=(d == NEIGHBOURS - 1),
                         is_transpose=True,
                     )
 
-        def mean_pairs(u, b, sums):
-            pair = keep.tile([P, 2 * P], BF16, name="pair", tag="pair%d_%d" % (u, b), align_bytes=64)
+        def mean_pairs(u, block, sums):
+            pair = keep.tile([P, 2 * P], BF16, name="pair", tag="pair%d_%d" % (u, block), align_bytes=64)
             nc.scalar.activation(
-                pair[:].rearrange("v (p e) -> v p e", e=2), sums[b][:].rearrange("v e p -> v p e"), COPY, scale=1.0 / 3.0
+                pair[:].rearrange("v (p e) -> v p e", e=2),
+                sums[block][:].rearrange("v e p -> v p e"),
+                COPY,
+                scale=1.0 / NEIGHBOURS,
             )
             return pair
 
-        def turn_back(b, pairs, z_half):
-            back = psum.tile([P, 2, P], F32, name="back", tag="acc", bufs=4)
+        def turn_back(block, pairs, z_half):
+            back = psum.tile([P, 2, P], F32, name="back", tag="ring", bufs=RING)
             for u in (1, 0):
                 nc.tensor.transpose(back[:, u, :], pairs[u][:].bitcast(F32), ident[:])
-            c = (b % 2) * P * PACK
+            c = (block % 2) * P * PACK
             nc.scalar.copy(
                 z_half[:, c : c + P * PACK].bitcast(F32).rearrange("p (v u) -> p v u", u=2),
                 back[:].rearrange("p u v -> p v u"),
             )
 
         def finish_means(blocks, sums, low_pairs, z_bf):
-            high_pairs = [mean_pairs(1, b, sums) for b in blocks]
-            for b, high in zip(blocks, high_pairs):
-                turn_back(b, (low_pairs[b], high), z_bf[b // 2])
+            high_pairs = [mean_pairs(1, block, sums) for block in blocks]
+            for block, high in zip(blocks, high_pairs):
+                turn_back(block, (low_pairs[block], high), z_bf[block // 2])
+
+        def sum_banks():
+            return [psum.tile([P, 2, P], F32, name="sums", tag="block%d" % block) for block in range(BLOCKS)]
 
         even = ("even0", "even1", "even2")
         odd = ("odd0", "odd1", "odd2")
-        sums = [psum.tile([P, 2, P], F32, name="sums", tag="sums%d" % b) for b in range(BLOCKS)]
+        sums = sum_banks()
         neighbours(0, 0, V, sums, even)
         neighbours(1, 0, V, sums, odd)
-        low_pairs = [mean_pairs(0, b, sums) for b in range(BLOCKS)]
-        sums = [psum.tile([P, 2, P], F32, name="sums", tag="sums%d" % b) for b in range(BLOCKS)]
+        low_pairs = [mean_pairs(0, block, sums) for block in range(BLOCKS)]
+        sums = sum_banks()
         neighbours(2, 0, V, sums, even)
         z_bf = [keep.tile([P, V // 2 * PACK], BF16, name="z_bf%d" % half, align_bytes=64) for half in range(2)]
         neighbours(3, 0, V - P, sums, odd)
         finish_means(range(BLOCKS - 1), sums, low_pairs, z_bf)
         neighbours(3, V - P, V, sums, even)
         finish_means(range(BLOCKS - 1, BLOCKS), sums, low_pairs, z_bf)
-        hc_bf = [centres(0, "odd0", "pair0_3"), centres(1, "odd1", "odd0"), centres(2, "odd2", "odd1")]
+
+        def centres(piece, gathered_tag, woven_tag):
+            a, b = CEN_PIECES[piece]
+            gathered = keep.tile([P, PACK, b - a], F32, name="gathered", tag=gathered_tag, align_bytes=64)
+            for t in range(PACK):
+                nc.vector.tensor_copy(gathered[:, t, :], h[t][:].indirect(entries(cen_list, a, b)))
+            woven = keep.tile([P, b - a, PACK], BF16, name="woven", tag=woven_tag, align_bytes=64)
+            nc.scalar.copy(
+                woven[:].rearrange("p (c n) t -> p c t n", n=4), gathered[:].rearrange("p t (c n) -> p c t n", n=4)
+            )
+            return woven
+
+        last_low, last_high = "pair0_%d" % (BLOCKS - 1), "pair1_%d" % (BLOCKS - 1)
+        hc_bf = [centres(0, odd[0], last_low), centres(1, odd[1], odd[0]), centres(2, odd[2], odd[1])]
 
         def neighbour_passes(half):
-            codes = keep.tile([P, V // 2], U32, name="z_codes", tag=("pair1_3", "z_codes1")[half], align_bytes=64)
+            codes = keep.tile([P, V // 2], U32, name="z_codes", tag=(last_high, "z_codes1")[half], align_bytes=64)
             plane = keep.tile([P, V // 2], U8, name="z_plane%d" % half, align_bytes=64)
             nc.vector.quantize_mx(out=codes[:].bitcast(FP8X4), scales=plane[:], in_=z_bf[half][:])
-            totals = []
+            opened = []
             for c in range(0, V // 2, P):
-                total = psum.tile([P, P], F32, name="total", tag="sums%d" % (2 * half + c // P))
+                total = psum.tile([P, P], F32, name="total", tag="block%d" % (2 * half + c // P))
                 nc.tensor.matmul_mx(
                     out=total[:],
                     lhsT=w3_codes[:].bitcast(FP4X4),
@@ -215,34 +231,34 @@ def tile_picked_sagecat_mean_p_kernel(
                     start=True,
                     stop=False,
                 )
-                totals.append(total)
-            return totals
+                opened.append(total)
+            return opened
 
-        def centre_passes(i, totals):
-            a, b = CEN_PIECES[i]
-            n = b - a
-            hc_codes = keep.tile([P, n], U32, name="hc_codes%d" % i, align_bytes=64)
-            hc_plane = keep.tile([P, n], U8, name="hc_plane%d" % i, align_bytes=64)
+        def centre_passes(piece, totals):
+            a, b = CEN_PIECES[piece]
+            codes = keep.tile([P, b - a], U32, name="hc_codes%d" % piece, align_bytes=64)
+            plane = keep.tile([P, b - a], U8, name="hc_plane%d" % piece, align_bytes=64)
             nc.vector.quantize_mx(
-                out=hc_codes[:].bitcast(FP8X4), scales=hc_plane[:], in_=hc_bf[i][:].rearrange("p n t -> p (n t)")
+                out=codes[:].bitcast(FP8X4), scales=plane[:], in_=hc_bf[piece][:].rearrange("p n t -> p (n t)")
             )
-            for c, total in zip(range(0, n, P), totals):
+            for c in range(a, b, P):
                 nc.tensor.matmul_mx(
-                    out=total[:],
+                    out=totals[c // P][:],
                     lhsT=w2_codes[:].bitcast(FP4X4),
                     lhsT_scale=w2_plane[:],
-                    rhs=hc_codes[:, c : c + P].bitcast(FP8X4),
-                    rhs_scale=hc_plane[:, c : c + P],
+                    rhs=codes[:, c - a : c - a + P].bitcast(FP8X4),
+                    rhs_scale=plane[:, c - a : c - a + P],
                     start=False,
                     stop=True,
                 )
 
         totals = neighbour_passes(0) + neighbour_passes(1)
-        centre_passes(0, totals[:2])
-        centre_passes(1, totals[2:3])
-        centre_passes(2, totals[3:])
-        for i, (a, b) in enumerate(CEN_PIECES):
-            result = keep.tile([P, b - a], F32, name="result", tag="odd2" if i == 0 else "result%d" % i, align_bytes=64)
+        for piece in range(len(CEN_PIECES)):
+            centre_passes(piece, totals)
+
+        for piece, (a, b) in enumerate(CEN_PIECES):
+            tag = odd[2] if piece == 0 else "result%d" % piece
+            result = keep.tile([P, b - a], F32, name="result", tag=tag, align_bytes=64)
             for c in range(a, b, P):
                 if c in (0, V - P):
                     nc.vector.tensor_copy(result[:, c - a : c - a + P], totals[c // P][:])

@@ -27,11 +27,11 @@ RING = 4
 ROW_STEP = P // 16
 ROW_FIRST = 4
 X_FIRST = 1024
-FIRST_ON_SCALAR = 40
 FIRST_PARTS = ((0, 256), (256, 512), (512, 768), (768, 896), (896, 1024))
 FIRST_ON_VECTOR = (2, 4)
-VECTOR_QUARTER = 2
-CAST_TAGS = ("w1_bf0", "w1_bf1", "w1_bf0", "w1_codes0")
+HOMES = P // 2
+TILE_ROWS = (((0,), 2, 4), ((1,), 2, 4), ((0, 1), 1, 2), ((0, 1), 0, 1))
+SUM_HALF = (0, 1, 1, 0)
 CEN_PIECES = ((0, 256), (256, 384), (384, 512))
 
 
@@ -74,12 +74,14 @@ def tile_picked_sagecat_mean_p_kernel(
         offs_list = load_list("offs_list", offs)
         nc.sync.dma_start(out=x_rows[ROW_FIRST:P:ROW_STEP, :].bitcast(I32), in_=x_scales[0].bitcast(I32))
         nc.sync.dma_start(out=x_table[:, X_FIRST:].bitcast(I32), in_=x_src[:, X_FIRST:])
-        w1_raw = keep.tile([P, PACK, H], F32, name="w1_raw")
-        nc.sync.dma_start(out=w1_raw[:], in_=w1.rearrange("(p j) c -> p j c", j=PACK))
+        w1_src = w1.rearrange("(p j) c -> p j c", j=PACK)
+        w1_halves = [keep.tile([P, PACK, H // 2], F32, name="w1_half%d" % half) for half in range(2)]
+        nc.sync.dma_start(out=w1_halves[0][:], in_=w1_src[:, :, : H // 2])
 
         picked_rows = keep.tile([P, S], U8, name="picked_rows")
         nc.vector.tensor_copy(picked_rows[:], x_rows[:].indirect(offs_list[:]))
         place_scale_rows(nc.sync, picked_plane, lambda r: picked_rows[ROW_FIRST + ROW_STEP * r : P : 32, :])
+        nc.sync.dma_start(out=w1_halves[1][:], in_=w1_src[:, :, H // 2 :])
 
         pos_lists = [load_list("pos%d_list" % d, src) for d, src in enumerate((pos1, pos2, pos3))]
         cen_list = load_list("cen_list", cen)
@@ -96,29 +98,28 @@ def tile_picked_sagecat_mean_p_kernel(
             nc.vector.tensor_copy(words[:], x_table[:].indirect(entries(offs_list, half * BANK, (half + 1) * BANK)))
             picked.append(words)
 
-        dealt = w1_raw[:].rearrange("p j (m t) -> p t m j", t=PACK)
-
-        def cast_w1(t):
-            w1_bf = keep.tile([P, P, PACK], BF16, name="w1_bf", tag=CAST_TAGS[t], align_bytes=64)
-            if t == 0:
-                nc.scalar.copy(w1_bf[:, :FIRST_ON_SCALAR], dealt[:, t, :FIRST_ON_SCALAR])
-                nc.vector.tensor_copy(w1_bf[:, FIRST_ON_SCALAR:], dealt[:, t, FIRST_ON_SCALAR:])
-            elif t == VECTOR_QUARTER:
-                nc.vector.tensor_copy(w1_bf[:], dealt[:, t])
-            else:
-                nc.scalar.copy(w1_bf[:], dealt[:, t])
-            return w1_bf
-
-        def quantise_w1(t, w1_bf):
-            codes = keep.tile([P, P], U32, name="w1_codes", tag="w1_codes%d" % t, align_bytes=64)
-            plane = keep.tile([P, P], U8, name="w1_plane%d" % t, align_bytes=64)
+        def weights(name, tiles, engine_copy, tag):
+            width = len(tiles) * P
+            w1_bf = keep.tile([P, width, PACK], BF16, name="w1_bf", tag=tag, align_bytes=64)
+            c = 0
+            for t in tiles:
+                halves, s0, s1 = TILE_ROWS[t]
+                for half in halves:
+                    count = HOMES * (s1 - s0)
+                    engine_copy(
+                        w1_bf[:, c : c + count, :].rearrange("p (q s) j -> p q j s", s=s1 - s0),
+                        w1_halves[half][:].rearrange("p j (q s) -> p q j s", s=PACK)[:, :, :, s0:s1],
+                    )
+                    c = c + count
+            codes = keep.tile([P, width], U32, name="codes", tag=name + "_codes", align_bytes=64)
+            plane = keep.tile([P, width], U8, name=name + "_plane", align_bytes=64)
             nc.vector.quantize_mx(
                 out=codes[:].bitcast(FP8X4), scales=plane[:], in_=w1_bf[:].rearrange("p m j -> p (m j)")
             )
-            return codes, plane
+            return [(codes[:, c : c + P], plane[:, c : c + P]) for c in range(0, width, P)]
 
         def hidden(t, codes, plane):
-            h_t = keep.tile([P, S], F32, name="h%d" % t)
+            h_t = keep.tile([P, S], F32, name="h_t", tag="h%d" % t, align_bytes=64)
             parts = FIRST_PARTS if t == 0 else ((0, BANK), (BANK, S))
             for part, (a, b) in enumerate(parts):
                 half = a // BANK
@@ -128,8 +129,8 @@ def tile_picked_sagecat_mean_p_kernel(
                     acc = psum.tile([P, b - a], F32, name="acc", tag="ring", bufs=RING)
                 nc.tensor.matmul_mx(
                     out=acc[:],
-                    lhsT=codes[:].bitcast(FP8X4),
-                    lhsT_scale=plane[:],
+                    lhsT=codes.bitcast(FP8X4),
+                    lhsT_scale=plane,
                     rhs=picked[half][:, a - half * BANK : b - half * BANK].bitcast(FP8X4),
                     rhs_scale=picked_plane[:, a:b],
                     start=True,
@@ -141,9 +142,18 @@ def tile_picked_sagecat_mean_p_kernel(
                     nc.scalar.activation(h_t[:, a:b], acc[:], RELU)
             return h_t
 
-        h = []
-        for t in range(PACK):
-            h.append(hidden(t, *quantise_w1(t, cast_w1(t))))
+        (w1_0,) = weights("w1_0", (0,), nc.scalar.copy, "w1_bf0")
+        h = [hidden(0, *w1_0)]
+        (w1_1,) = weights("w1_1", (1,), nc.vector.tensor_copy, "w1_bf0")
+        w1_2, w1_3 = weights("w1_2", (2, 3), nc.scalar.copy, "w1_0_codes")
+        h = h + [hidden(1, *w1_1), hidden(2, *w1_2), hidden(3, *w1_3)]
+
+        slots = [h[3], h[2]]
+        for e in range(2):
+            moved = keep.tile([P, S], F32, name="moved", tag="slot%d" % (2 + e), align_bytes=64)
+            for half in range(2):
+                nc.sync.dma_start(out=moved[half * HOMES : (half + 1) * HOMES, :], in_=h[half][e:P:2, :])
+            slots.append(moved)
 
         def neighbours(t, a, b, sums, tags):
             for d in range(NEIGHBOURS):
@@ -151,7 +161,7 @@ def tile_picked_sagecat_mean_p_kernel(
                 nc.vector.tensor_copy(got[:], h[t][:].indirect(entries(pos_lists[d], a, b)))
                 for c in range(a, b, P):
                     nc.tensor.matmul(
-                        sums[c // P][:, t % 2, :],
+                        sums[c // P][:, SUM_HALF[t], :],
                         got[:, c - a : c - a + P],
                         ident[:],
                         start=(d == 0),
@@ -161,18 +171,17 @@ def tile_picked_sagecat_mean_p_kernel(
 
         def mean_pairs(u, block, sums):
             pair = keep.tile([P, 2 * P], BF16, name="pair", tag="pair%d_%d" % (u, block), align_bytes=64)
-            nc.scalar.activation(
-                pair[:].rearrange("v (p e) -> v p e", e=2),
-                sums[block][:].rearrange("v e p -> v p e"),
-                COPY,
-                scale=1.0 / NEIGHBOURS,
-            )
+            if u == 0:
+                src = sums[block][:].rearrange("v t (q e) -> v (t q) e", e=2)
+            else:
+                src = sums[block][:].rearrange("v e p -> v p e")
+            nc.scalar.activation(pair[:].rearrange("v (p e) -> v p e", e=2), src, COPY, scale=1.0 / NEIGHBOURS)
             return pair
 
         def turn_back(block, pairs, z_half):
             back = psum.tile([P, 2, P], F32, name="back", tag="ring", bufs=RING)
             for u in (1, 0):
-                nc.tensor.transpose(back[:, u, :], pairs[u][:].bitcast(F32), ident[:])
+                nc.tensor.transpose(back[:, 1 - u, :], pairs[u][:].bitcast(F32), ident[:])
             c = (block % 2) * P * PACK
             nc.scalar.copy(
                 z_half[:, c : c + P * PACK].bitcast(F32).rearrange("p (v u) -> p v u", u=2),
@@ -201,23 +210,34 @@ def tile_picked_sagecat_mean_p_kernel(
         neighbours(3, V - P, V, sums, even)
         finish_means(range(BLOCKS - 1, BLOCKS), sums, low_pairs, z_bf)
 
-        def centres(piece, gathered_tag, woven_tag):
-            a, b = CEN_PIECES[piece]
-            gathered = keep.tile([P, PACK, b - a], F32, name="gathered", tag=gathered_tag, align_bytes=64)
-            for t in range(PACK):
-                nc.vector.tensor_copy(gathered[:, t, :], h[t][:].indirect(entries(cen_list, a, b)))
-            woven = keep.tile([P, b - a, PACK], BF16, name="woven", tag=woven_tag, align_bytes=64)
+        def fetch(slot, a, b, dst):
+            nc.vector.tensor_copy(dst, slots[slot][:].indirect(entries(cen_list, a, b)))
+
+        def weave(woven, gathered):
             nc.scalar.copy(
-                woven[:].rearrange("p (c n) t -> p c t n", n=4), gathered[:].rearrange("p t (c n) -> p c t n", n=4)
+                woven.rearrange("p (c n) t -> p c t n", n=4), gathered.rearrange("p t (c n) -> p c t n", n=4)
             )
-            return woven
 
         last_low, last_high = "pair0_%d" % (BLOCKS - 1), "pair1_%d" % (BLOCKS - 1)
-        hc_bf = [centres(0, odd[0], last_low), centres(1, odd[1], odd[0]), centres(2, odd[2], odd[1])]
+        half = V // 2
+        first_found = keep.tile([P, PACK, half], F32, name="first_found", tag=odd[0], align_bytes=64)
+        for slot in range(PACK):
+            fetch(slot, 0, half, first_found[:, slot, :])
+        first_woven = keep.tile([P, half, PACK], BF16, name="first_woven", tag=last_low, align_bytes=64)
+        weave(first_woven[:], first_found[:])
+        second_found = keep.tile([P, PACK, half], F32, name="second_found", tag="h1", align_bytes=64)
+        second_woven = keep.tile([P, half, PACK], BF16, name="second_woven", tag=odd[0], align_bytes=64)
+        for slot in range(2):
+            fetch(slot, half, V, second_found[:, slot, :])
+        for c in range(0, half, P):
+            for slot in range(2, PACK):
+                fetch(slot, half + c, half + c + P, second_found[:, slot, c : c + P])
+            weave(second_woven[:, c : c + P, :], second_found[:, :, c : c + P])
+        hc_bf = [first_woven[:], second_woven[:, :P, :], second_woven[:, P:, :]]
 
         def neighbour_passes(half):
             codes = keep.tile([P, V // 2], U32, name="z_codes", tag=(last_high, "z_codes1")[half], align_bytes=64)
-            plane = keep.tile([P, V // 2], U8, name="z_plane%d" % half, align_bytes=64)
+            plane = keep.tile([P, V // 2], U8, name="z_plane", tag="slot%d" % (3 - half), align_bytes=64)
             nc.vector.quantize_mx(out=codes[:].bitcast(FP8X4), scales=plane[:], in_=z_bf[half][:])
             opened = []
             for c in range(0, V // 2, P):
@@ -239,7 +259,7 @@ def tile_picked_sagecat_mean_p_kernel(
             codes = keep.tile([P, b - a], U32, name="hc_codes%d" % piece, align_bytes=64)
             plane = keep.tile([P, b - a], U8, name="hc_plane%d" % piece, align_bytes=64)
             nc.vector.quantize_mx(
-                out=codes[:].bitcast(FP8X4), scales=plane[:], in_=hc_bf[piece][:].rearrange("p n t -> p (n t)")
+                out=codes[:].bitcast(FP8X4), scales=plane[:], in_=hc_bf[piece].rearrange("p n t -> p (n t)")
             )
             for c in range(a, b, P):
                 nc.tensor.matmul_mx(
@@ -257,7 +277,7 @@ def tile_picked_sagecat_mean_p_kernel(
             centre_passes(piece, totals)
 
         for piece, (a, b) in enumerate(CEN_PIECES):
-            tag = odd[2] if piece == 0 else "result%d" % piece
+            tag = "h1" if piece == 0 else "result%d" % piece
             result = keep.tile([P, b - a], F32, name="result", tag=tag, align_bytes=64)
             for c in range(a, b, P):
                 if c in (0, V - P):

@@ -28,7 +28,7 @@ ROW_STEP = P // 16
 ROW_FIRST = 4
 X_FIRST = 1024
 FIRST_PARTS = ((0, 256), (256, 512), (512, 768), (768, 896), (896, 1024))
-FIRST_ON_VECTOR = (2, 4)
+FIRST_ON_VECTOR = ()
 HOMES = P // 2
 TILE_ROWS = (((0,), 2, 4), ((1,), 2, 4), ((0, 1), 1, 2), ((0, 1), 0, 1))
 SUM_HALF = (0, 1, 1, 0)
@@ -98,7 +98,7 @@ def tile_picked_sagecat_mean_p_kernel(
             nc.vector.tensor_copy(words[:], x_table[:].indirect(entries(offs_list, half * BANK, (half + 1) * BANK)))
             picked.append(words)
 
-        def weights(name, tiles, engine_copy, tag):
+        def weights(name, tiles, tag):
             width = len(tiles) * P
             w1_bf = keep.tile([P, width, PACK], BF16, name="w1_bf", tag=tag, align_bytes=64)
             c = 0
@@ -106,7 +106,7 @@ def tile_picked_sagecat_mean_p_kernel(
                 halves, s0, s1 = TILE_ROWS[t]
                 for half in halves:
                     count = HOMES * (s1 - s0)
-                    engine_copy(
+                    (nc.scalar.copy, nc.vector.tensor_copy)[half](
                         w1_bf[:, c : c + count, :].rearrange("p (q s) j -> p q j s", s=s1 - s0),
                         w1_halves[half][:].rearrange("p j (q s) -> p q j s", s=PACK)[:, :, :, s0:s1],
                     )
@@ -142,10 +142,10 @@ def tile_picked_sagecat_mean_p_kernel(
                     nc.scalar.activation(h_t[:, a:b], acc[:], RELU)
             return h_t
 
-        (w1_0,) = weights("w1_0", (0,), nc.scalar.copy, "w1_bf0")
+        (w1_0,) = weights("w1_0", (0,), "w1_bf0")
         h = [hidden(0, *w1_0)]
-        (w1_1,) = weights("w1_1", (1,), nc.vector.tensor_copy, "w1_bf0")
-        w1_2, w1_3 = weights("w1_2", (2, 3), nc.scalar.copy, "w1_0_codes")
+        (w1_1,) = weights("w1_1", (1,), "w1_bf0")
+        w1_2, w1_3 = weights("w1_2", (2, 3), "w1_bf2")
         h = h + [hidden(1, *w1_1), hidden(2, *w1_2), hidden(3, *w1_3)]
 
         slots = [h[3], h[2]]

@@ -23,16 +23,18 @@ BANK = 512
 LIST_ROWS = 16
 NEIGHBOURS = 3
 BLOCKS = V // P
-RING = 4
 ROW_STEP = P // 16
 ROW_FIRST = 4
 X_FIRST = 1024
 FIRST_PARTS = ((0, 256), (256, 512), (512, 768), (768, 896), (896, 1024))
-FIRST_ON_VECTOR = ()
 HOMES = P // 2
 TILE_ROWS = (((0,), 2, 4), ((1,), 2, 4), ((0, 1), 1, 2), ((0, 1), 0, 1))
 SUM_HALF = (0, 1, 1, 0)
-CEN_PIECES = ((0, 256), (256, 384), (384, 512))
+PIECES = ((0, 256), (256, 384), (384, 512))
+H_BANKS = ((0, 1, 2, 3, 4), (5, 6), (7, 0), (1, 2))
+EARLY_BANKS = (3, 4, 5, 6)
+LATE_BANKS = (7, 0, 1, 2)
+ON_SCALAR = ((1, 1), (2, 0), (2, 2), (3, 1))
 
 
 def tile_picked_sagecat_mean_p_kernel(
@@ -118,15 +120,15 @@ def tile_picked_sagecat_mean_p_kernel(
             )
             return [(codes[:, c : c + P], plane[:, c : c + P]) for c in range(0, width, P)]
 
+        def bank(name, shape, number):
+            return psum.tile(shape, F32, name=name, tag="bank%d" % number)
+
         def hidden(t, codes, plane):
             h_t = keep.tile([P, S], F32, name="h_t", tag="h%d" % t, align_bytes=64)
             parts = FIRST_PARTS if t == 0 else ((0, BANK), (BANK, S))
             for part, (a, b) in enumerate(parts):
                 half = a // BANK
-                if t == 0 and part > 0:
-                    acc = psum.tile([P, b - a], F32, name="acc", tag="block%d" % (part - 1))
-                else:
-                    acc = psum.tile([P, b - a], F32, name="acc", tag="ring", bufs=RING)
+                acc = bank("acc", [P, b - a], H_BANKS[t][part])
                 nc.tensor.matmul_mx(
                     out=acc[:],
                     lhsT=codes.bitcast(FP8X4),
@@ -136,10 +138,7 @@ def tile_picked_sagecat_mean_p_kernel(
                     start=True,
                     stop=True,
                 )
-                if t == 0 and part in FIRST_ON_VECTOR:
-                    nc.vector.tensor_scalar_max(h_t[:, a:b], acc[:], 0.0)
-                else:
-                    nc.scalar.activation(h_t[:, a:b], acc[:], RELU)
+                nc.scalar.activation(h_t[:, a:b], acc[:], RELU)
             return h_t
 
         (w1_0,) = weights("w1_0", (0,), "w1_bf0")
@@ -155,14 +154,20 @@ def tile_picked_sagecat_mean_p_kernel(
                 nc.sync.dma_start(out=moved[half * HOMES : (half + 1) * HOMES, :], in_=h[half][e:P:2, :])
             slots.append(moved)
 
-        def neighbours(t, a, b, sums, tags):
+        def gather(on_scalar, dst, window, offsets):
+            if on_scalar:
+                nc.scalar.activation(dst, window.indirect(offsets), COPY)
+            else:
+                nc.vector.tensor_copy(dst, window.indirect(offsets))
+
+        def neighbours(t, sums):
             for d in range(NEIGHBOURS):
-                got = keep.tile([P, b - a], F32, name="got", tag=tags[d], align_bytes=64)
-                nc.vector.tensor_copy(got[:], h[t][:].indirect(entries(pos_lists[d], a, b)))
-                for c in range(a, b, P):
+                got = keep.tile([P, V], F32, name="got", tag="got%d_%d" % (t, d), align_bytes=64)
+                gather((t, d) in ON_SCALAR, got[:], h[t][:], pos_lists[d][:])
+                for c in range(0, V, P):
                     nc.tensor.matmul(
                         sums[c // P][:, SUM_HALF[t], :],
-                        got[:, c - a : c - a + P],
+                        got[:, c : c + P],
                         ident[:],
                         start=(d == 0),
                         stop=(d == NEIGHBOURS - 1),
@@ -178,110 +183,76 @@ def tile_picked_sagecat_mean_p_kernel(
             nc.scalar.activation(pair[:].rearrange("v (p e) -> v p e", e=2), src, COPY, scale=1.0 / NEIGHBOURS)
             return pair
 
-        def turn_back(block, pairs, z_half):
-            back = psum.tile([P, 2, P], F32, name="back", tag="ring", bufs=RING)
-            for u in (1, 0):
-                nc.tensor.transpose(back[:, 1 - u, :], pairs[u][:].bitcast(F32), ident[:])
-            c = (block % 2) * P * PACK
-            nc.scalar.copy(
-                z_half[:, c : c + P * PACK].bitcast(F32).rearrange("p (v u) -> p v u", u=2),
-                back[:].rearrange("p u v -> p v u"),
-            )
+        early_sums = [bank("sums", [P, 2, P], EARLY_BANKS[block]) for block in range(BLOCKS)]
+        late_sums = [bank("sums", [P, 2, P], LATE_BANKS[block]) for block in range(BLOCKS)]
+        neighbours(0, early_sums)
+        neighbours(1, early_sums)
+        neighbours(2, late_sums)
+        neighbours(3, late_sums)
+        early_pairs = [mean_pairs(0, block, early_sums) for block in range(BLOCKS)]
 
-        def finish_means(blocks, sums, low_pairs, z_bf):
-            high_pairs = [mean_pairs(1, block, sums) for block in blocks]
-            for block, high in zip(blocks, high_pairs):
-                turn_back(block, (low_pairs[block], high), z_bf[block // 2])
-
-        def sum_banks():
-            return [psum.tile([P, 2, P], F32, name="sums", tag="block%d" % block) for block in range(BLOCKS)]
-
-        even = ("even0", "even1", "even2")
-        odd = ("odd0", "odd1", "odd2")
-        sums = sum_banks()
-        neighbours(0, 0, V, sums, even)
-        neighbours(1, 0, V, sums, odd)
-        low_pairs = [mean_pairs(0, block, sums) for block in range(BLOCKS)]
-        sums = sum_banks()
-        neighbours(2, 0, V, sums, even)
-        z_bf = [keep.tile([P, V // 2 * PACK], BF16, name="z_bf%d" % half, align_bytes=64) for half in range(2)]
-        neighbours(3, 0, V - P, sums, odd)
-        finish_means(range(BLOCKS - 1), sums, low_pairs, z_bf)
-        neighbours(3, V - P, V, sums, even)
-        finish_means(range(BLOCKS - 1, BLOCKS), sums, low_pairs, z_bf)
-
-        def fetch(slot, a, b, dst):
-            nc.vector.tensor_copy(dst, slots[slot][:].indirect(entries(cen_list, a, b)))
-
-        def weave(woven, gathered):
-            nc.scalar.copy(
-                woven.rearrange("p (c n) t -> p c t n", n=4), gathered.rearrange("p t (c n) -> p c t n", n=4)
-            )
-
-        last_low, last_high = "pair0_%d" % (BLOCKS - 1), "pair1_%d" % (BLOCKS - 1)
-        half = V // 2
-        first_found = keep.tile([P, PACK, half], F32, name="first_found", tag=odd[0], align_bytes=64)
+        found = keep.tile([P, PACK, V], F32, name="found", tag="got2_0", align_bytes=64)
         for slot in range(PACK):
-            fetch(slot, 0, half, first_found[:, slot, :])
-        first_woven = keep.tile([P, half, PACK], BF16, name="first_woven", tag=last_low, align_bytes=64)
-        weave(first_woven[:], first_found[:])
-        second_found = keep.tile([P, PACK, half], F32, name="second_found", tag="h1", align_bytes=64)
-        second_woven = keep.tile([P, half, PACK], BF16, name="second_woven", tag=odd[0], align_bytes=64)
-        for slot in range(2):
-            fetch(slot, half, V, second_found[:, slot, :])
-        for c in range(0, half, P):
-            for slot in range(2, PACK):
-                fetch(slot, half + c, half + c + P, second_found[:, slot, c : c + P])
-            weave(second_woven[:, c : c + P, :], second_found[:, :, c : c + P])
-        hc_bf = [first_woven[:], second_woven[:, :P, :], second_woven[:, P:, :]]
-
-        def neighbour_passes(half):
-            codes = keep.tile([P, V // 2], U32, name="z_codes", tag=(last_high, "z_codes1")[half], align_bytes=64)
-            plane = keep.tile([P, V // 2], U8, name="z_plane", tag="slot%d" % (3 - half), align_bytes=64)
-            nc.vector.quantize_mx(out=codes[:].bitcast(FP8X4), scales=plane[:], in_=z_bf[half][:])
-            opened = []
-            for c in range(0, V // 2, P):
-                total = psum.tile([P, P], F32, name="total", tag="block%d" % (2 * half + c // P))
-                nc.tensor.matmul_mx(
-                    out=total[:],
-                    lhsT=w3_codes[:].bitcast(FP4X4),
-                    lhsT_scale=w3_plane[:],
-                    rhs=codes[:, c : c + P].bitcast(FP8X4),
-                    rhs_scale=plane[:, c : c + P],
-                    start=True,
-                    stop=False,
-                )
-                opened.append(total)
-            return opened
-
-        def centre_passes(piece, totals):
-            a, b = CEN_PIECES[piece]
-            codes = keep.tile([P, b - a], U32, name="hc_codes%d" % piece, align_bytes=64)
-            plane = keep.tile([P, b - a], U8, name="hc_plane%d" % piece, align_bytes=64)
-            nc.vector.quantize_mx(
-                out=codes[:].bitcast(FP8X4), scales=plane[:], in_=hc_bf[piece].rearrange("p n t -> p (n t)")
+            gather(slot < 2, found[:, slot, :], slots[slot][:], cen_list[:])
+        woven = []
+        for half in range(2):
+            tile = keep.tile([P, V // 2, PACK], BF16, name="woven", tag="woven%d" % half, align_bytes=64)
+            nc.vector.tensor_copy(
+                tile[:].rearrange("p (c n) t -> p c t n", n=4),
+                found[:, :, half * V // 2 : (half + 1) * V // 2].rearrange("p t (c n) -> p c t n", n=4),
             )
+            woven.append(tile)
+        hc_codes = keep.tile([P, V], U32, name="hc_codes", align_bytes=64)
+        hc_plane = keep.tile([P, V], U8, name="hc_plane", align_bytes=64)
+        for half in range(2):
+            cols = slice(half * V // 2, (half + 1) * V // 2)
+            nc.vector.quantize_mx(
+                out=hc_codes[:, cols].bitcast(FP8X4),
+                scales=hc_plane[:, cols],
+                in_=woven[half][:].rearrange("p n t -> p (n t)"),
+            )
+
+        late_pairs = [mean_pairs(1, block, late_sums) for block in range(BLOCKS)]
+        z_bf = [
+            keep.tile([P, (b - a) * PACK], BF16, name="z_bf%d" % a, align_bytes=64) for a, b in PIECES
+        ]
+        for piece, (a, b) in enumerate(PIECES):
             for c in range(a, b, P):
-                nc.tensor.matmul_mx(
-                    out=totals[c // P][:],
-                    lhsT=w2_codes[:].bitcast(FP4X4),
-                    lhsT_scale=w2_plane[:],
-                    rhs=codes[:, c - a : c - a + P].bitcast(FP8X4),
-                    rhs_scale=plane[:, c - a : c - a + P],
-                    start=False,
-                    stop=True,
+                block = c // P
+                back = bank("back", [P, 2, P], EARLY_BANKS[block])
+                nc.tensor.transpose(back[:, 0, :], late_pairs[block][:].bitcast(F32), ident[:])
+                nc.tensor.transpose(back[:, 1, :], early_pairs[block][:].bitcast(F32), ident[:])
+                nc.scalar.copy(
+                    z_bf[piece][:, (c - a) * PACK : (c - a + P) * PACK].bitcast(F32).rearrange("p (v u) -> p v u", u=2),
+                    back[:].rearrange("p u v -> p v u"),
                 )
 
-        totals = neighbour_passes(0) + neighbour_passes(1)
-        for piece in range(len(CEN_PIECES)):
-            centre_passes(piece, totals)
-
-        for piece, (a, b) in enumerate(CEN_PIECES):
-            tag = "h1" if piece == 0 else "result%d" % piece
-            result = keep.tile([P, b - a], F32, name="result", tag=tag, align_bytes=64)
-            for c in range(a, b, P):
-                if c in (0, V - P):
-                    nc.vector.tensor_copy(result[:, c - a : c - a + P], totals[c // P][:])
-                else:
-                    nc.scalar.copy(result[:, c - a : c - a + P], totals[c // P][:])
+        for piece, (a, b) in enumerate(PIECES):
+            codes = keep.tile([P, b - a], U32, name="z_codes", tag=("woven0", "got2_0", "slot3")[piece], align_bytes=64)
+            plane = keep.tile([P, b - a], U8, name="z_plane%d" % piece, align_bytes=64)
+            nc.vector.quantize_mx(out=codes[:].bitcast(FP8X4), scales=plane[:], in_=z_bf[piece][:])
+            total = bank("total", [P, b - a], EARLY_BANKS[b // P - 1])
+            nc.tensor.matmul_mx(
+                out=total[:],
+                lhsT=w2_codes[:].bitcast(FP4X4),
+                lhsT_scale=w2_plane[:],
+                rhs=hc_codes[:, a:b].bitcast(FP8X4),
+                rhs_scale=hc_plane[:, a:b],
+                start=True,
+                stop=False,
+            )
+            nc.tensor.matmul_mx(
+                out=total[:],
+                lhsT=w3_codes[:].bitcast(FP4X4),
+                lhsT_scale=w3_plane[:],
+                rhs=codes[:].bitcast(FP8X4),
+                rhs_scale=plane[:],
+                start=False,
+                stop=True,
+            )
+            result = keep.tile([P, b - a], F32, name="result%d" % piece, align_bytes=64)
+            if piece == len(PIECES) - 1:
+                nc.vector.tensor_copy(result[:], total[:])
+            else:
+                nc.scalar.copy(result[:], total[:])
             nc.sync.dma_start(out=out[:, a:b], in_=result[:])

@@ -32,8 +32,10 @@ TILE_ROWS = (((0,), 2, 4), ((1,), 2, 4), ((0, 1), 1, 2), ((0, 1), 0, 1))
 SUM_HALF = (0, 1, 1, 0)
 PIECES = ((0, 256), (256, 384), (384, 512))
 H_BANKS = ((0, 1, 2, 3, 4), (5, 6), (7, 0), (1, 2))
-EARLY_BANKS = (3, 4, 5, 6)
-LATE_BANKS = (7, 0, 1, 2)
+CUT = 768
+EARLY_BANKS = (3, 4)
+LATE_BANKS = (5, 6)
+BACK_BANKS = (7, 0, 1)
 ON_SCALAR = ((1, 1), (2, 0), (2, 2), (3, 1))
 
 
@@ -94,11 +96,12 @@ def tile_picked_sagecat_mean_p_kernel(
         place_scale_rows(nc.sync, w3_plane, lambda r: w3_scales[0, r:16:4, :])
         place_scale_rows(nc.sync, w2_plane, lambda r: w2_scales[0, r:16:4, :])
 
-        picked = []
-        for half in range(S // BANK):
-            words = keep.tile([P, BANK], U32, name="picked%d" % half, align_bytes=64)
-            nc.vector.tensor_copy(words[:], x_table[:].indirect(entries(offs_list, half * BANK, (half + 1) * BANK)))
-            picked.append(words)
+        def pick(a, b, tag):
+            words = keep.tile([P, b - a], U32, name="picked", tag=tag, align_bytes=64)
+            nc.vector.tensor_copy(words[:], x_table[:].indirect(entries(offs_list, a, b)))
+            return words
+
+        first_words = pick(0, CUT, "first_words")
 
         def weights(name, tiles, tag):
             width = len(tiles) * P
@@ -127,23 +130,25 @@ def tile_picked_sagecat_mean_p_kernel(
             h_t = keep.tile([P, S], F32, name="h_t", tag="h%d" % t, align_bytes=64)
             parts = FIRST_PARTS if t == 0 else ((0, BANK), (BANK, S))
             for part, (a, b) in enumerate(parts):
-                half = a // BANK
                 acc = bank("acc", [P, b - a], H_BANKS[t][part])
-                nc.tensor.matmul_mx(
-                    out=acc[:],
-                    lhsT=codes.bitcast(FP8X4),
-                    lhsT_scale=plane,
-                    rhs=picked[half][:, a - half * BANK : b - half * BANK].bitcast(FP8X4),
-                    rhs_scale=picked_plane[:, a:b],
-                    start=True,
-                    stop=True,
-                )
+                for c, d in ((a, CUT), (CUT, b)) if a < CUT < b else ((a, b),):
+                    words = first_words[:, c:d] if d <= CUT else last_words[:, c - CUT : d - CUT]
+                    nc.tensor.matmul_mx(
+                        out=acc[:, c - a : d - a],
+                        lhsT=codes.bitcast(FP8X4),
+                        lhsT_scale=plane,
+                        rhs=words.bitcast(FP8X4),
+                        rhs_scale=picked_plane[:, c:d],
+                        start=True,
+                        stop=True,
+                    )
                 nc.scalar.activation(h_t[:, a:b], acc[:], RELU)
             return h_t
 
         (w1_0,) = weights("w1_0", (0,), "w1_bf0")
+        last_words = pick(CUT, S, "w1_bf0")
         h = [hidden(0, *w1_0)]
-        (w1_1,) = weights("w1_1", (1,), "w1_bf0")
+        (w1_1,) = weights("w1_1", (1,), "w1_bf1")
         w1_2, w1_3 = weights("w1_2", (2, 3), "w1_bf2")
         h = h + [hidden(1, *w1_1), hidden(2, *w1_2), hidden(3, *w1_3)]
 
@@ -165,41 +170,45 @@ def tile_picked_sagecat_mean_p_kernel(
                 got = keep.tile([P, V], F32, name="got", tag="got%d_%d" % (t, d), align_bytes=64)
                 gather((t, d) in ON_SCALAR, got[:], h[t][:], pos_lists[d][:])
                 for c in range(0, V, P):
+                    block = c // P
                     nc.tensor.matmul(
-                        sums[c // P][:, SUM_HALF[t], :],
+                        sums[block // 2][:, block % 2, SUM_HALF[t], :],
                         got[:, c : c + P],
                         ident[:],
-                        start=(d == 0),
-                        stop=(d == NEIGHBOURS - 1),
+                        start=(t % 2 == 0 and d == 0 and block % 2 == 0),
+                        stop=(t % 2 == 1 and d == NEIGHBOURS - 1 and block % 2 == 1),
                         is_transpose=True,
                     )
 
-        def mean_pairs(u, block, sums):
-            pair = keep.tile([P, 2 * P], BF16, name="pair", tag="pair%d_%d" % (u, block), align_bytes=64)
+        def mean_pairs(u, half, sums):
+            pair = keep.tile([P, 2, 2 * P], BF16, name="pair", tag="pair%d_%d" % (u, half), align_bytes=64)
             if u == 0:
-                src = sums[block][:].rearrange("v t (q e) -> v (t q) e", e=2)
+                src = sums[half][:].rearrange("v b t (q e) -> v b (t q) e", e=2)
             else:
-                src = sums[block][:].rearrange("v e p -> v p e")
-            nc.scalar.activation(pair[:].rearrange("v (p e) -> v p e", e=2), src, COPY, scale=1.0 / NEIGHBOURS)
-            return pair
+                src = sums[half][:].rearrange("v b e p -> v b p e")
+            nc.scalar.activation(pair[:].rearrange("v b (p e) -> v b p e", e=2), src, COPY, scale=1.0 / NEIGHBOURS)
+            return [pair[:, 0, :], pair[:, 1, :]]
 
-        early_sums = [bank("sums", [P, 2, P], EARLY_BANKS[block]) for block in range(BLOCKS)]
-        late_sums = [bank("sums", [P, 2, P], LATE_BANKS[block]) for block in range(BLOCKS)]
+        early_sums = [bank("sums", [P, 2, 2, P], EARLY_BANKS[half]) for half in range(2)]
+        late_sums = [bank("sums", [P, 2, 2, P], LATE_BANKS[half]) for half in range(2)]
         neighbours(0, early_sums)
         neighbours(1, early_sums)
         neighbours(2, late_sums)
         neighbours(3, late_sums)
-        early_pairs = [mean_pairs(0, block, early_sums) for block in range(BLOCKS)]
+        early_pairs = mean_pairs(0, 0, early_sums) + mean_pairs(0, 1, early_sums)
 
-        found = keep.tile([P, PACK, V], F32, name="found", tag="got2_0", align_bytes=64)
-        for slot in range(PACK):
-            gather(slot < 2, found[:, slot, :], slots[slot][:], cen_list[:])
+        found = keep.tile([P, PACK, V], BF16, name="found", tag="got2_0", align_bytes=64)
+        gather(True, found[:, 0, :], slots[0][:], cen_list[:])
+        gather(True, found[:, 1, : V // 2], slots[1][:], entries(cen_list, 0, V // 2))
+        gather(False, found[:, 2, :], slots[2][:], cen_list[:])
+        gather(False, found[:, 3, :], slots[3][:], cen_list[:])
+        gather(False, found[:, 1, V // 2 :], slots[1][:], entries(cen_list, V // 2, V))
         woven = []
         for half in range(2):
             tile = keep.tile([P, V // 2, PACK], BF16, name="woven", tag="woven%d" % half, align_bytes=64)
             nc.vector.tensor_copy(
-                tile[:].rearrange("p (c n) t -> p c t n", n=4),
-                found[:, :, half * V // 2 : (half + 1) * V // 2].rearrange("p t (c n) -> p c t n", n=4),
+                tile[:],
+                found[:, :, half * V // 2 : (half + 1) * V // 2].rearrange("p t n -> p n t"),
             )
             woven.append(tile)
         hc_codes = keep.tile([P, V], U32, name="hc_codes", align_bytes=64)
@@ -212,26 +221,25 @@ def tile_picked_sagecat_mean_p_kernel(
                 in_=woven[half][:].rearrange("p n t -> p (n t)"),
             )
 
-        late_pairs = [mean_pairs(1, block, late_sums) for block in range(BLOCKS)]
+        late_pairs = mean_pairs(1, 0, late_sums) + mean_pairs(1, 1, late_sums)
         z_bf = [
             keep.tile([P, (b - a) * PACK], BF16, name="z_bf%d" % a, align_bytes=64) for a, b in PIECES
         ]
         for piece, (a, b) in enumerate(PIECES):
+            back = bank("back", [P, 2, b - a], BACK_BANKS[piece])
             for c in range(a, b, P):
-                block = c // P
-                back = bank("back", [P, 2, P], EARLY_BANKS[block])
-                nc.tensor.transpose(back[:, 0, :], late_pairs[block][:].bitcast(F32), ident[:])
-                nc.tensor.transpose(back[:, 1, :], early_pairs[block][:].bitcast(F32), ident[:])
-                nc.scalar.copy(
-                    z_bf[piece][:, (c - a) * PACK : (c - a + P) * PACK].bitcast(F32).rearrange("p (v u) -> p v u", u=2),
-                    back[:].rearrange("p u v -> p v u"),
-                )
+                nc.tensor.transpose(back[:, 0, c - a : c - a + P], late_pairs[c // P].bitcast(F32), ident[:])
+                nc.tensor.transpose(back[:, 1, c - a : c - a + P], early_pairs[c // P].bitcast(F32), ident[:])
+            nc.scalar.copy(
+                z_bf[piece][:].bitcast(F32).rearrange("p (v u) -> p v u", u=2),
+                back[:].rearrange("p u v -> p v u"),
+            )
 
         for piece, (a, b) in enumerate(PIECES):
             codes = keep.tile([P, b - a], U32, name="z_codes", tag=("woven0", "got2_0", "slot3")[piece], align_bytes=64)
             plane = keep.tile([P, b - a], U8, name="z_plane%d" % piece, align_bytes=64)
             nc.vector.quantize_mx(out=codes[:].bitcast(FP8X4), scales=plane[:], in_=z_bf[piece][:])
-            total = bank("total", [P, b - a], EARLY_BANKS[b // P - 1])
+            total = bank("total", [P, b - a], BACK_BANKS[piece])
             nc.tensor.matmul_mx(
                 out=total[:],
                 lhsT=w2_codes[:].bitcast(FP4X4),

@@ -197,7 +197,7 @@ def tile_picked_sagecat_mean_p_kernel(
         neighbours(3, late_sums)
         early_pairs = mean_pairs(0, 0, early_sums) + mean_pairs(0, 1, early_sums)
 
-        found = keep.tile([P, PACK, V], BF16, name="found", tag="got2_0", align_bytes=64)
+        found = keep.tile([P, PACK, V], F32, name="found", tag="got2_0", align_bytes=64)
         gather(True, found[:, 0, :], slots[0][:], cen_list[:])
         gather(True, found[:, 1, : V // 2], slots[1][:], entries(cen_list, 0, V // 2))
         gather(False, found[:, 2, :], slots[2][:], cen_list[:])
@@ -207,8 +207,8 @@ def tile_picked_sagecat_mean_p_kernel(
         for half in range(2):
             tile = keep.tile([P, V // 2, PACK], BF16, name="woven", tag="woven%d" % half, align_bytes=64)
             nc.vector.tensor_copy(
-                tile[:],
-                found[:, :, half * V // 2 : (half + 1) * V // 2].rearrange("p t n -> p n t"),
+                tile[:].rearrange("p (c n) t -> p c t n", n=4),
+                found[:, :, half * V // 2 : (half + 1) * V // 2].rearrange("p t (c n) -> p c t n", n=4),
             )
             woven.append(tile)
         hc_codes = keep.tile([P, V], U32, name="hc_codes", align_bytes=64)

@@ -1,7 +1,6 @@
 from contextlib import ExitStack
 
 import concourse.mybir as mybir
-from concourse.masks import make_identity
 
 K, T, S, V, H, N = 512, 4096, 1024, 512, 512, 128
 FLOPS = 2 * K * H * S + 2 * 2 * H * N * V
@@ -16,6 +15,7 @@ FP8X4 = mybir.dt.float8_e4m3fn_x4
 FP4X4 = mybir.dt.float4_e2m1fn_x4
 COPY = mybir.ActivationFunctionType.Copy
 RELU = mybir.ActivationFunctionType.Relu
+ADD = mybir.AluOpType.add
 
 P = 128
 PACK = 4
@@ -26,16 +26,18 @@ BLOCKS = V // P
 ROW_STEP = P // 16
 ROW_FIRST = 4
 X_FIRST = 1024
-FIRST_PARTS = ((0, 256), (256, 512), (512, 768), (768, 896), (896, 1024))
+FIRST_PARTS = ((0, 512), (512, 768), (768, 1024))
 HOMES = P // 2
-TILE_ROWS = (((0,), 2, 4), ((1,), 2, 4), ((0, 1), 1, 2), ((0, 1), 0, 1))
+TILE_ROWS = (((0, 1), 0, 1), ((0, 1), 1, 2), ((0, 1), 2, 3), ((0, 1), 3, 4))
 SUM_HALF = (0, 1, 1, 0)
 PIECES = ((0, 256), (256, 384), (384, 512))
-H_BANKS = ((0, 1, 2, 3, 4), (5, 6), (7, 0), (1, 2))
-CUT = 768
+H_BANKS = ((0, 1, 2), (3, 4), (5, 6), (7, 0))
+CUT = 512
+CAST_ON_VECTOR = 32
+HALVES = ((0, 256), (256, 512))
 EARLY_BANKS = (3, 4)
 LATE_BANKS = (5, 6)
-BACK_BANKS = (7, 0, 1)
+TOTAL_BANKS = (1, 2, 3)
 ON_SCALAR = ((1, 1), (2, 0), (2, 2), (3, 1))
 
 
@@ -68,10 +70,6 @@ def tile_picked_sagecat_mean_p_kernel(
         nc.vector.memset(w2_plane[:].bitcast(I32), 0)
         nc.vector.memset(w3_plane[:].bitcast(I32), 0)
 
-        ident = keep.tile([P, P], F32, name="ident")
-        nc.vector.memset(ident[:], 0.0)
-        make_identity(nc, ident[:], nomemset=True)
-
         x_table = keep.tile([P, T], U32, name="x_table")
         x_src = x_words[0].rearrange("p n t -> p (n t)").bitcast(I32)
         nc.sync.dma_start(out=x_table[:, :X_FIRST].bitcast(I32), in_=x_src[:, :X_FIRST])
@@ -81,11 +79,11 @@ def tile_picked_sagecat_mean_p_kernel(
         w1_src = w1.rearrange("(p j) c -> p j c", j=PACK)
         w1_halves = [keep.tile([P, PACK, H // 2], F32, name="w1_half%d" % half) for half in range(2)]
         nc.sync.dma_start(out=w1_halves[0][:], in_=w1_src[:, :, : H // 2])
+        nc.sync.dma_start(out=w1_halves[1][:], in_=w1_src[:, :, H // 2 :])
 
         picked_rows = keep.tile([P, S], U8, name="picked_rows")
         nc.vector.tensor_copy(picked_rows[:], x_rows[:].indirect(offs_list[:]))
         place_scale_rows(nc.sync, picked_plane, lambda r: picked_rows[ROW_FIRST + ROW_STEP * r : P : 32, :])
-        nc.sync.dma_start(out=w1_halves[1][:], in_=w1_src[:, :, H // 2 :])
 
         pos_lists = [load_list("pos%d_list" % d, src) for d, src in enumerate((pos1, pos2, pos3))]
         cen_list = load_list("cen_list", cen)
@@ -102,24 +100,25 @@ def tile_picked_sagecat_mean_p_kernel(
             return words
 
         first_words = pick(0, CUT, "first_words")
+        last_words = pick(CUT, S, "last_words")
 
-        def weights(name, tiles, tag):
-            width = len(tiles) * P
-            w1_bf = keep.tile([P, width, PACK], BF16, name="w1_bf", tag=tag, align_bytes=64)
-            c = 0
-            for t in tiles:
-                halves, s0, s1 = TILE_ROWS[t]
-                for half in halves:
-                    count = HOMES * (s1 - s0)
-                    (nc.scalar.copy, nc.vector.tensor_copy)[half](
-                        w1_bf[:, c : c + count, :].rearrange("p (q s) j -> p q j s", s=s1 - s0),
-                        w1_halves[half][:].rearrange("p j (q s) -> p q j s", s=PACK)[:, :, :, s0:s1],
-                    )
-                    c = c + count
+        w1_bf = keep.tile([P, PACK, P, PACK], BF16, name="w1_bf", align_bytes=64)
+
+        def cast(copy, half, a, b, t0, t1):
+            copy(
+                w1_bf[:, t0:t1, half * HOMES + a : half * HOMES + b, :].rearrange("p t q j -> p q t j"),
+                w1_halves[half][:].rearrange("p j (q t) -> p q t j", t=PACK)[:, a:b, t0:t1, :],
+            )
+
+        cast(nc.scalar.copy, 0, 0, HOMES, 0, PACK)
+        cast(nc.vector.tensor_copy, 1, 0, HOMES, 0, 1)
+
+        def weights(name, a, b):
+            width = (b - a) * P
             codes = keep.tile([P, width], U32, name="codes", tag=name + "_codes", align_bytes=64)
             plane = keep.tile([P, width], U8, name=name + "_plane", align_bytes=64)
             nc.vector.quantize_mx(
-                out=codes[:].bitcast(FP8X4), scales=plane[:], in_=w1_bf[:].rearrange("p m j -> p (m j)")
+                out=codes[:].bitcast(FP8X4), scales=plane[:], in_=w1_bf[:, a:b].rearrange("p t m j -> p (t m j)")
             )
             return [(codes[:, c : c + P], plane[:, c : c + P]) for c in range(0, width, P)]
 
@@ -142,22 +141,11 @@ def tile_picked_sagecat_mean_p_kernel(
                         start=True,
                         stop=True,
                     )
-                nc.scalar.activation(h_t[:, a:b], acc[:], RELU)
+                if t == 0 and part > 0:
+                    nc.vector.tensor_scalar_max(h_t[:, a:b], acc[:], 0.0)
+                else:
+                    nc.scalar.activation(h_t[:, a:b], acc[:], RELU)
             return h_t
-
-        (w1_0,) = weights("w1_0", (0,), "w1_bf0")
-        last_words = pick(CUT, S, "w1_bf0")
-        h = [hidden(0, *w1_0)]
-        (w1_1,) = weights("w1_1", (1,), "w1_bf1")
-        w1_2, w1_3 = weights("w1_2", (2, 3), "w1_bf2")
-        h = h + [hidden(1, *w1_1), hidden(2, *w1_2), hidden(3, *w1_3)]
-
-        slots = [h[3], h[2]]
-        for e in range(2):
-            moved = keep.tile([P, S], F32, name="moved", tag="slot%d" % (2 + e), align_bytes=64)
-            for half in range(2):
-                nc.sync.dma_start(out=moved[half * HOMES : (half + 1) * HOMES, :], in_=h[half][e:P:2, :])
-            slots.append(moved)
 
         def gather(on_scalar, dst, window, offsets):
             if on_scalar:
@@ -165,94 +153,88 @@ def tile_picked_sagecat_mean_p_kernel(
             else:
                 nc.vector.tensor_copy(dst, window.indirect(offsets))
 
-        def neighbours(t, sums):
-            for d in range(NEIGHBOURS):
-                got = keep.tile([P, V], F32, name="got", tag="got%d_%d" % (t, d), align_bytes=64)
-                gather((t, d) in ON_SCALAR, got[:], h[t][:], pos_lists[d][:])
-                for c in range(0, V, P):
-                    block = c // P
-                    nc.tensor.matmul(
-                        sums[block // 2][:, block % 2, SUM_HALF[t], :],
-                        got[:, c : c + P],
-                        ident[:],
-                        start=(t % 2 == 0 and d == 0 and block % 2 == 0),
-                        stop=(t % 2 == 1 and d == NEIGHBOURS - 1 and block % 2 == 1),
-                        is_transpose=True,
-                    )
+        sums = keep.tile([P, PACK, V], F32, name="sums", align_bytes=64)
 
-        def mean_pairs(u, half, sums):
-            pair = keep.tile([P, 2, 2 * P], BF16, name="pair", tag="pair%d_%d" % (u, half), align_bytes=64)
-            if u == 0:
-                src = sums[half][:].rearrange("v b t (q e) -> v b (t q) e", e=2)
+        def first_neighbours(t):
+            one = keep.tile([P, V], F32, name="one%d" % t, align_bytes=64)
+            if t == 0:
+                gather(False, one[:, : V // 2], h[t][:], entries(pos_lists[0], 0, V // 2))
+                gather(True, one[:, V // 2 :], h[t][:], entries(pos_lists[0], V // 2, V))
             else:
-                src = sums[half][:].rearrange("v b e p -> v b p e")
-            nc.scalar.activation(pair[:].rearrange("v b (p e) -> v b p e", e=2), src, COPY, scale=1.0 / NEIGHBOURS)
-            return [pair[:, 0, :], pair[:, 1, :]]
+                gather(True, one[:], h[t][:], pos_lists[0][:])
+            return one
 
-        early_sums = [bank("sums", [P, 2, 2, P], EARLY_BANKS[half]) for half in range(2)]
-        late_sums = [bank("sums", [P, 2, 2, P], LATE_BANKS[half]) for half in range(2)]
-        neighbours(0, early_sums)
-        neighbours(1, early_sums)
-        neighbours(2, late_sums)
-        neighbours(3, late_sums)
-        early_pairs = mean_pairs(0, 0, early_sums) + mean_pairs(0, 1, early_sums)
+        def add_neighbours(t, one):
+            two = keep.tile([P, V], F32, name="two%d" % t, align_bytes=64)
+            for d, src, dst in ((1, one[:], two[:]), (2, two[:], sums[:, t, :])):
+                for a, b in HALVES:
+                    nc.vector.tensor_tensor(dst[:, a:b], h[t][:].indirect(entries(pos_lists[d], a, b)), src[:, a:b], ADD)
 
-        found = keep.tile([P, PACK, V], F32, name="found", tag="got2_0", align_bytes=64)
-        gather(True, found[:, 0, :], slots[0][:], cen_list[:])
-        gather(True, found[:, 1, : V // 2], slots[1][:], entries(cen_list, 0, V // 2))
-        gather(False, found[:, 2, :], slots[2][:], cen_list[:])
-        gather(False, found[:, 3, :], slots[3][:], cen_list[:])
-        gather(False, found[:, 1, V // 2 :], slots[1][:], entries(cen_list, V // 2, V))
-        woven = []
-        for half in range(2):
-            tile = keep.tile([P, V // 2, PACK], BF16, name="woven", tag="woven%d" % half, align_bytes=64)
-            nc.vector.tensor_copy(
-                tile[:].rearrange("p (c n) t -> p c t n", n=4),
-                found[:, :, half * V // 2 : (half + 1) * V // 2].rearrange("p t (c n) -> p c t n", n=4),
+        (w1_0,) = weights("w1_0", 0, 1)
+        cast(nc.vector.tensor_copy, 1, 0, CAST_ON_VECTOR, 1, PACK)
+        cast(nc.scalar.copy, 1, CAST_ON_VECTOR, HOMES, 1, PACK)
+        w1_1, w1_2, w1_3 = weights("w1_1", 1, 4)
+        h = [hidden(0, *w1_0)]
+        ones = [first_neighbours(0)]
+        for t, w in ((1, w1_1), (2, w1_2), (3, w1_3)):
+            h.append(hidden(t, *w))
+            ones.append(first_neighbours(t))
+        for t in range(PACK):
+            add_neighbours(t, ones[t])
+
+        found = []
+        for half, (a, b) in enumerate(HALVES):
+            tile = keep.tile([P, PACK, b - a], F32, name="found", tag="one%d" % (1 + half), align_bytes=64)
+            for slot in range(PACK):
+                gather(True, tile[:, slot, :], h[slot][:], entries(cen_list, a, b))
+            found.append(tile)
+
+        def woven_views(tile, src, a, b):
+            return (
+                tile.rearrange("p (c n) t -> p c t n", n=4),
+                src[:, :, a:b].rearrange("p t (c n) -> p c t n", n=4),
             )
-            woven.append(tile)
-        hc_codes = keep.tile([P, V], U32, name="hc_codes", align_bytes=64)
-        hc_plane = keep.tile([P, V], U8, name="hc_plane", align_bytes=64)
+
+        def quantise(tile, codes, plane):
+            nc.vector.quantize_mx(out=codes.bitcast(FP8X4), scales=plane, in_=tile[:].rearrange("p n t -> p (n t)"))
+
+        z_codes = keep.tile([P, V], U32, name="z_codes", align_bytes=64)
+        z_plane = keep.tile([P, V], U8, name="z_plane", align_bytes=64)
+        z_bf = []
+        for half in range(2):
+            tile = keep.tile([P, V // 2, PACK], BF16, name="z_bf%d" % half, align_bytes=64)
+            nc.vector.tensor_scalar_mul(*woven_views(tile[:], sums, half * V // 2, (half + 1) * V // 2), 1.0 / NEIGHBOURS)
+            z_bf.append(tile)
         for half in range(2):
             cols = slice(half * V // 2, (half + 1) * V // 2)
-            nc.vector.quantize_mx(
-                out=hc_codes[:, cols].bitcast(FP8X4),
-                scales=hc_plane[:, cols],
-                in_=woven[half][:].rearrange("p n t -> p (n t)"),
-            )
+            quantise(z_bf[half], z_codes[:, cols], z_plane[:, cols])
 
-        late_pairs = mean_pairs(1, 0, late_sums) + mean_pairs(1, 1, late_sums)
-        z_bf = [
-            keep.tile([P, (b - a) * PACK], BF16, name="z_bf%d" % a, align_bytes=64) for a, b in PIECES
+        woven = [
+            keep.tile([P, b - a, PACK], BF16, name="woven%d" % a, align_bytes=64) for a, b in PIECES
         ]
-        for piece, (a, b) in enumerate(PIECES):
-            back = bank("back", [P, 2, b - a], BACK_BANKS[piece])
-            for c in range(a, b, P):
-                nc.tensor.transpose(back[:, 0, c - a : c - a + P], late_pairs[c // P].bitcast(F32), ident[:])
-                nc.tensor.transpose(back[:, 1, c - a : c - a + P], early_pairs[c // P].bitcast(F32), ident[:])
-            nc.scalar.copy(
-                z_bf[piece][:].bitcast(F32).rearrange("p (v u) -> p v u", u=2),
-                back[:].rearrange("p u v -> p v u"),
-            )
+        blocks = (woven[0][:, :P, :], woven[0][:, P:, :], woven[1][:], woven[2][:])
+        for block in range(BLOCKS):
+            c = block % 2 * P
+            (nc.scalar.copy, nc.vector.tensor_copy)[block % 2](*woven_views(blocks[block], found[block // 2], c, c + P))
 
         for piece, (a, b) in enumerate(PIECES):
-            codes = keep.tile([P, b - a], U32, name="z_codes", tag=("woven0", "got2_0", "slot3")[piece], align_bytes=64)
-            plane = keep.tile([P, b - a], U8, name="z_plane%d" % piece, align_bytes=64)
-            nc.vector.quantize_mx(out=codes[:].bitcast(FP8X4), scales=plane[:], in_=z_bf[piece][:])
-            total = bank("total", [P, b - a], BACK_BANKS[piece])
+            codes = keep.tile([P, b - a], U32, name="hc_codes%d" % piece, align_bytes=64)
+            plane = keep.tile([P, b - a], U8, name="hc_plane%d" % piece, align_bytes=64)
+            quantise(woven[piece], codes[:], plane[:])
+            total = bank("total", [P, b - a], TOTAL_BANKS[piece])
             nc.tensor.matmul_mx(
                 out=total[:],
-                lhsT=w2_codes[:].bitcast(FP4X4),
-                lhsT_scale=w2_plane[:],
-                rhs=hc_codes[:, a:b].bitcast(FP8X4),
-                rhs_scale=hc_plane[:, a:b],
+                lhsT=w3_codes[:].bitcast(FP4X4),
+                lhsT_scale=w3_plane[:],
+                rhs=z_codes[:, a:b].bitcast(FP8X4),
+                rhs_scale=z_plane[:, a:b],
                 start=True,
                 stop=False,
             )
             nc.tensor.matmul_mx(
                 out=total[:],
-                lhsT=w3_codes[:].bitcast(FP4X4),
-                lhsT_scale=w3_plane[:],
+                lhsT=w2_codes[:].bitcast(FP4X4),
+                lhsT_scale=w2_plane[:],
                 rhs=codes[:].bitcast(FP8X4),
                 rhs_scale=plane[:],
                 start=False,

@@ -19,26 +19,13 @@ ADD = mybir.AluOpType.add
 
 P = 128
 PACK = 4
-BANK = 512
 LIST_ROWS = 16
 NEIGHBOURS = 3
-BLOCKS = V // P
 ROW_STEP = P // 16
 ROW_FIRST = 4
-X_FIRST = 1024
-FIRST_PARTS = ((0, 512), (512, 768), (768, 1024))
-HOMES = P // 2
-TILE_ROWS = (((0, 1), 0, 1), ((0, 1), 1, 2), ((0, 1), 2, 3), ((0, 1), 3, 4))
-SUM_HALF = (0, 1, 1, 0)
-PIECES = ((0, 256), (256, 384), (384, 512))
-H_BANKS = ((0, 1, 2), (3, 4), (5, 6), (7, 0))
-CUT = 512
-CAST_ON_VECTOR = 32
+WORD_PIECES = ((0, 256), (256, 768), (768, 1024))
 HALVES = ((0, 256), (256, 512))
-EARLY_BANKS = (3, 4)
-LATE_BANKS = (5, 6)
-TOTAL_BANKS = (1, 2, 3)
-ON_SCALAR = ((1, 1), (2, 0), (2, 2), (3, 1))
+PIECES = ((0, 256), (384, 512), (256, 384))
 
 
 def tile_picked_sagecat_mean_p_kernel(
@@ -57,9 +44,9 @@ def tile_picked_sagecat_mean_p_kernel(
         def entries(list_tile, a, b):
             return list_tile[:, a // LIST_ROWS : b // LIST_ROWS]
 
-        def place_scale_rows(queue, plane, rows):
+        def place_scale_rows(plane, rows):
             for r in range(4):
-                queue.dma_start(out=plane[r:P:32, :].bitcast(I32), in_=rows(r).bitcast(I32))
+                nc.sync.dma_start(out=plane[r:P:32, :].bitcast(I32), in_=rows(r).bitcast(I32))
 
         x_rows = keep.tile([P, T], U8, name="x_rows")
         nc.vector.memset(x_rows[:].bitcast(I32), 0)
@@ -70,20 +57,16 @@ def tile_picked_sagecat_mean_p_kernel(
         nc.vector.memset(w2_plane[:].bitcast(I32), 0)
         nc.vector.memset(w3_plane[:].bitcast(I32), 0)
 
-        x_table = keep.tile([P, T], U32, name="x_table")
-        x_src = x_words[0].rearrange("p n t -> p (n t)").bitcast(I32)
-        nc.sync.dma_start(out=x_table[:, :X_FIRST].bitcast(I32), in_=x_src[:, :X_FIRST])
+        w1_raw = keep.tile([P, PACK, H], F32, name="w1_raw")
+        nc.sync.dma_start(out=w1_raw[:], in_=w1.rearrange("(p j) c -> p j c", j=PACK))
         offs_list = load_list("offs_list", offs)
         nc.sync.dma_start(out=x_rows[ROW_FIRST:P:ROW_STEP, :].bitcast(I32), in_=x_scales[0].bitcast(I32))
-        nc.sync.dma_start(out=x_table[:, X_FIRST:].bitcast(I32), in_=x_src[:, X_FIRST:])
-        w1_src = w1.rearrange("(p j) c -> p j c", j=PACK)
-        w1_halves = [keep.tile([P, PACK, H // 2], F32, name="w1_half%d" % half) for half in range(2)]
-        nc.sync.dma_start(out=w1_halves[0][:], in_=w1_src[:, :, : H // 2])
-        nc.sync.dma_start(out=w1_halves[1][:], in_=w1_src[:, :, H // 2 :])
+        x_table = keep.tile([P, T], U32, name="x_table")
+        nc.sync.dma_start(out=x_table[:].bitcast(I32), in_=x_words[0].rearrange("p n t -> p (n t)").bitcast(I32))
 
         picked_rows = keep.tile([P, S], U8, name="picked_rows")
         nc.vector.tensor_copy(picked_rows[:], x_rows[:].indirect(offs_list[:]))
-        place_scale_rows(nc.sync, picked_plane, lambda r: picked_rows[ROW_FIRST + ROW_STEP * r : P : 32, :])
+        place_scale_rows(picked_plane, lambda r: picked_rows[ROW_FIRST + ROW_STEP * r : P : 32, :])
 
         pos_lists = [load_list("pos%d_list" % d, src) for d, src in enumerate((pos1, pos2, pos3))]
         cen_list = load_list("cen_list", cen)
@@ -91,61 +74,49 @@ def tile_picked_sagecat_mean_p_kernel(
         w3_codes = keep.tile([P, 2 * N], U8, name="w3_codes", align_bytes=64)
         nc.sync.dma_start(out=w3_codes[:].bitcast(I32), in_=w3_words[0].bitcast(I32))
         nc.sync.dma_start(out=w2_codes[:].bitcast(I32), in_=w2_words[0].bitcast(I32))
-        place_scale_rows(nc.sync, w3_plane, lambda r: w3_scales[0, r:16:4, :])
-        place_scale_rows(nc.sync, w2_plane, lambda r: w2_scales[0, r:16:4, :])
-
-        def pick(a, b, tag):
-            words = keep.tile([P, b - a], U32, name="picked", tag=tag, align_bytes=64)
-            nc.vector.tensor_copy(words[:], x_table[:].indirect(entries(offs_list, a, b)))
-            return words
-
-        first_words = pick(0, CUT, "first_words")
-        last_words = pick(CUT, S, "last_words")
+        place_scale_rows(w3_plane, lambda r: w3_scales[0, r:16:4, :])
+        place_scale_rows(w2_plane, lambda r: w2_scales[0, r:16:4, :])
 
         w1_bf = keep.tile([P, PACK, P, PACK], BF16, name="w1_bf", align_bytes=64)
+        nc.scalar.copy(
+            w1_bf[:].rearrange("p t q j -> p q t j"), w1_raw[:].rearrange("p j (q t) -> p q t j", t=PACK)
+        )
+        w1_codes = keep.tile([P, H], U32, name="w1_codes", align_bytes=64)
+        w1_plane = keep.tile([P, H], U8, name="w1_plane", align_bytes=64)
+        nc.vector.quantize_mx(
+            out=w1_codes[:].bitcast(FP8X4), scales=w1_plane[:], in_=w1_bf[:].rearrange("p t m j -> p (t m j)")
+        )
 
-        def cast(copy, half, a, b, t0, t1):
-            copy(
-                w1_bf[:, t0:t1, half * HOMES + a : half * HOMES + b, :].rearrange("p t q j -> p q t j"),
-                w1_halves[half][:].rearrange("p j (q t) -> p q t j", t=PACK)[:, a:b, t0:t1, :],
+        words = []
+        for a, b in WORD_PIECES:
+            tile = keep.tile([P, b - a], U32, name="words%d" % a, align_bytes=64)
+            nc.vector.tensor_copy(tile[:], x_table[:].indirect(entries(offs_list, a, b)))
+            words.append(tile)
+
+        def bank(number):
+            return psum.tile([P, 512], F32, name="bank", tag="bank%d" % number)
+
+        h = [keep.tile([P, S], F32, name="h%d" % t, align_bytes=64) for t in range(PACK)]
+
+        def product(t, acc, a, b):
+            piece = max(i for i, (c, d) in enumerate(WORD_PIECES) if c <= a)
+            first = WORD_PIECES[piece][0]
+            cols = slice(t * P, (t + 1) * P)
+            nc.tensor.matmul_mx(
+                out=acc,
+                lhsT=w1_codes[:, cols].bitcast(FP8X4),
+                lhsT_scale=w1_plane[:, cols],
+                rhs=words[piece][:, a - first : b - first].bitcast(FP8X4),
+                rhs_scale=picked_plane[:, a:b],
+                start=True,
+                stop=True,
             )
 
-        cast(nc.scalar.copy, 0, 0, HOMES, 0, PACK)
-        cast(nc.vector.tensor_copy, 1, 0, HOMES, 0, 1)
-
-        def weights(name, a, b):
-            width = (b - a) * P
-            codes = keep.tile([P, width], U32, name="codes", tag=name + "_codes", align_bytes=64)
-            plane = keep.tile([P, width], U8, name=name + "_plane", align_bytes=64)
-            nc.vector.quantize_mx(
-                out=codes[:].bitcast(FP8X4), scales=plane[:], in_=w1_bf[:, a:b].rearrange("p t m j -> p (t m j)")
-            )
-            return [(codes[:, c : c + P], plane[:, c : c + P]) for c in range(0, width, P)]
-
-        def bank(name, shape, number):
-            return psum.tile(shape, F32, name=name, tag="bank%d" % number)
-
-        def hidden(t, codes, plane):
-            h_t = keep.tile([P, S], F32, name="h_t", tag="h%d" % t, align_bytes=64)
-            parts = FIRST_PARTS if t == 0 else ((0, BANK), (BANK, S))
-            for part, (a, b) in enumerate(parts):
-                acc = bank("acc", [P, b - a], H_BANKS[t][part])
-                for c, d in ((a, CUT), (CUT, b)) if a < CUT < b else ((a, b),):
-                    words = first_words[:, c:d] if d <= CUT else last_words[:, c - CUT : d - CUT]
-                    nc.tensor.matmul_mx(
-                        out=acc[:, c - a : d - a],
-                        lhsT=codes.bitcast(FP8X4),
-                        lhsT_scale=plane,
-                        rhs=words.bitcast(FP8X4),
-                        rhs_scale=picked_plane[:, c:d],
-                        start=True,
-                        stop=True,
-                    )
-                if t == 0 and part > 0:
-                    nc.vector.tensor_scalar_max(h_t[:, a:b], acc[:], 0.0)
-                else:
-                    nc.scalar.activation(h_t[:, a:b], acc[:], RELU)
-            return h_t
+        def relu(on_scalar, t, acc, a, b):
+            if on_scalar:
+                nc.scalar.activation(h[t][:, a:b], acc, RELU)
+            else:
+                nc.vector.tensor_scalar_max(h[t][:, a:b], acc, 0.0)
 
         def gather(on_scalar, dst, window, offsets):
             if on_scalar:
@@ -153,41 +124,66 @@ def tile_picked_sagecat_mean_p_kernel(
             else:
                 nc.vector.tensor_copy(dst, window.indirect(offsets))
 
-        sums = keep.tile([P, PACK, V], F32, name="sums", align_bytes=64)
-
-        def first_neighbours(t):
-            one = keep.tile([P, V], F32, name="one%d" % t, align_bytes=64)
-            if t == 0:
-                gather(False, one[:, : V // 2], h[t][:], entries(pos_lists[0], 0, V // 2))
-                gather(True, one[:, V // 2 :], h[t][:], entries(pos_lists[0], V // 2, V))
-            else:
-                gather(True, one[:], h[t][:], pos_lists[0][:])
-            return one
-
-        def add_neighbours(t, one):
-            two = keep.tile([P, V], F32, name="two%d" % t, align_bytes=64)
-            for d, src, dst in ((1, one[:], two[:]), (2, two[:], sums[:, t, :])):
-                for a, b in HALVES:
-                    nc.vector.tensor_tensor(dst[:, a:b], h[t][:].indirect(entries(pos_lists[d], a, b)), src[:, a:b], ADD)
-
-        (w1_0,) = weights("w1_0", 0, 1)
-        cast(nc.vector.tensor_copy, 1, 0, CAST_ON_VECTOR, 1, PACK)
-        cast(nc.scalar.copy, 1, CAST_ON_VECTOR, HOMES, 1, PACK)
-        w1_1, w1_2, w1_3 = weights("w1_1", 1, 4)
-        h = [hidden(0, *w1_0)]
-        ones = [first_neighbours(0)]
-        for t, w in ((1, w1_1), (2, w1_2), (3, w1_3)):
-            h.append(hidden(t, *w))
-            ones.append(first_neighbours(t))
+        narrow = [bank(t) for t in range(PACK)]
         for t in range(PACK):
-            add_neighbours(t, ones[t])
+            product(t, narrow[t][:, :256], 0, 256)
+        for t in range(3):
+            relu(True, t, narrow[t][:, :256], 0, 256)
+        relu(False, 3, narrow[3][:, :256], 0, 256)
+        for part, (a, b) in enumerate(((256, 512), (512, 768), (768, 896), (896, 1024))):
+            acc = bank(PACK + part)
+            product(0, acc[:, : b - a], a, b)
+            relu(part < 3, 0, acc[:, : b - a], a, b)
 
-        found = []
-        for half, (a, b) in enumerate(HALVES):
-            tile = keep.tile([P, PACK, b - a], F32, name="found", tag="one%d" % (1 + half), align_bytes=64)
-            for slot in range(PACK):
-                gather(True, tile[:, slot, :], h[slot][:], entries(cen_list, a, b))
-            found.append(tile)
+        sums = keep.tile([P, PACK, V], F32, name="sums", align_bytes=64)
+        ones = [keep.tile([P, V], F32, name="one%d" % t, align_bytes=64) for t in range(PACK - 1)]
+        ones.append(sums[:, 2, :])
+        gather(False, ones[0][:, : V // 2], h[0][:], entries(pos_lists[0], 0, V // 2))
+        gather(True, ones[0][:, V // 2 :], h[0][:], entries(pos_lists[0], V // 2, V))
+        wide = [None]
+        for t in range(1, PACK):
+            wide.append(bank(PACK + t - 1))
+            product(t, wide[t][:], 256, 768)
+            product(t, narrow[t][:, 256:], 768, 1024)
+
+        def rest(t, part):
+            if part == 0:
+                relu(True, t, wide[t][:], 256, 768)
+            else:
+                relu(True, t, narrow[t][:, 256:], 768, 1024)
+
+        def first(t):
+            gather(True, ones[t][:, :], h[t][:], pos_lists[0][:])
+
+        rest(1, 0)
+        rest(1, 1)
+        rest(2, 0)
+        first(1)
+        rest(2, 1)
+        rest(3, 0)
+        rest(3, 1)
+        first(2)
+        first(3)
+
+        twos = [keep.tile([P, V], F32, name="two%d" % t, align_bytes=64) for t in range(PACK)]
+
+        def add(t, d, a, b):
+            src, dst = ((ones[t], twos[t]), (twos[t], sums[:, t, :]))[d - 1]
+            nc.vector.tensor_tensor(dst[:, a:b], h[t][:].indirect(entries(pos_lists[d], a, b)), src[:, a:b], ADD)
+
+        for t in (0, 1):
+            for d in (1, 2):
+                for a, b in reversed(HALVES) if t == 0 else HALVES:
+                    add(t, d, a, b)
+        add(2, 1, 0, V)
+        add(3, 1, 0, V)
+        add(2, 2, 0, V)
+        for a, b in HALVES:
+            add(3, 2, a, b)
+
+        found = keep.tile([P, PACK, V], F32, name="found", align_bytes=64)
+        for slot in range(PACK):
+            gather(True, found[:, slot, :], h[slot][:], cen_list[:])
 
         def woven_views(tile, src, a, b):
             return (
@@ -209,21 +205,17 @@ def tile_picked_sagecat_mean_p_kernel(
             cols = slice(half * V // 2, (half + 1) * V // 2)
             quantise(z_bf[half], z_codes[:, cols], z_plane[:, cols])
 
-        woven = [
-            keep.tile([P, b - a, PACK], BF16, name="woven%d" % a, align_bytes=64) for a, b in PIECES
-        ]
-        blocks = (woven[0][:, :P, :], woven[0][:, P:, :], woven[1][:], woven[2][:])
-        for block in range(BLOCKS):
-            c = block % 2 * P
-            (nc.scalar.copy, nc.vector.tensor_copy)[block % 2](*woven_views(blocks[block], found[block // 2], c, c + P))
+        woven = [keep.tile([P, b - a, PACK], BF16, name="woven%d" % a, align_bytes=64) for a, b in PIECES]
+        for piece, (a, b) in enumerate(PIECES):
+            (nc.scalar.copy, nc.vector.tensor_copy)[piece % 2](*woven_views(woven[piece][:], found, a, b))
 
         for piece, (a, b) in enumerate(PIECES):
             codes = keep.tile([P, b - a], U32, name="hc_codes%d" % piece, align_bytes=64)
             plane = keep.tile([P, b - a], U8, name="hc_plane%d" % piece, align_bytes=64)
             quantise(woven[piece], codes[:], plane[:])
-            total = bank("total", [P, b - a], TOTAL_BANKS[piece])
+            total = bank(piece)
             nc.tensor.matmul_mx(
-                out=total[:],
+                out=total[:, : b - a],
                 lhsT=w3_codes[:].bitcast(FP4X4),
                 lhsT_scale=w3_plane[:],
                 rhs=z_codes[:, a:b].bitcast(FP8X4),
@@ -232,7 +224,7 @@ def tile_picked_sagecat_mean_p_kernel(
                 stop=False,
             )
             nc.tensor.matmul_mx(
-                out=total[:],
+                out=total[:, : b - a],
                 lhsT=w2_codes[:].bitcast(FP4X4),
                 lhsT_scale=w2_plane[:],
                 rhs=codes[:].bitcast(FP8X4),
@@ -241,8 +233,8 @@ def tile_picked_sagecat_mean_p_kernel(
                 stop=True,
             )
             result = keep.tile([P, b - a], F32, name="result%d" % piece, align_bytes=64)
-            if piece == len(PIECES) - 1:
-                nc.vector.tensor_copy(result[:], total[:])
+            if piece == 1:
+                nc.vector.tensor_copy(result[:], total[:, : b - a])
             else:
-                nc.scalar.copy(result[:], total[:])
+                nc.scalar.copy(result[:], total[:, : b - a])
             nc.sync.dma_start(out=out[:, a:b], in_=result[:])

@@ -25,7 +25,8 @@ ROW_STEP = P // 16
 ROW_FIRST = 4
 WORD_PIECES = ((0, 256), (256, 768), (768, 1024))
 HALVES = ((0, 256), (256, 512))
-PIECES = ((0, 256), (384, 512), (256, 384))
+PIECES = ((0, 128), (128, 256), (384, 512), (256, 384))
+WEAVE_CUT = 320
 
 
 def tile_picked_sagecat_mean_p_kernel(
@@ -136,8 +137,7 @@ def tile_picked_sagecat_mean_p_kernel(
             relu(part < 3, 0, acc[:, : b - a], a, b)
 
         sums = keep.tile([P, PACK, V], F32, name="sums", align_bytes=64)
-        ones = [keep.tile([P, V], F32, name="one%d" % t, align_bytes=64) for t in range(PACK - 1)]
-        ones.append(sums[:, 2, :])
+        ones = [keep.tile([P, V], F32, name="one%d" % t, align_bytes=64) for t in range(PACK)]
         gather(False, ones[0][:, : V // 2], h[0][:], entries(pos_lists[0], 0, V // 2))
         gather(True, ones[0][:, V // 2 :], h[0][:], entries(pos_lists[0], V // 2, V))
         wide = [None]
@@ -192,7 +192,7 @@ def tile_picked_sagecat_mean_p_kernel(
             )
 
         def quantise(tile, codes, plane):
-            nc.vector.quantize_mx(out=codes.bitcast(FP8X4), scales=plane, in_=tile[:].rearrange("p n t -> p (n t)"))
+            nc.vector.quantize_mx(out=codes.bitcast(FP8X4), scales=plane, in_=tile.rearrange("p n t -> p (n t)"))
 
         z_codes = keep.tile([P, V], U32, name="z_codes", align_bytes=64)
         z_plane = keep.tile([P, V], U8, name="z_plane", align_bytes=64)
@@ -203,19 +203,22 @@ def tile_picked_sagecat_mean_p_kernel(
             z_bf.append(tile)
         for half in range(2):
             cols = slice(half * V // 2, (half + 1) * V // 2)
-            quantise(z_bf[half], z_codes[:, cols], z_plane[:, cols])
+            quantise(z_bf[half][:], z_codes[:, cols], z_plane[:, cols])
 
-        woven = [keep.tile([P, b - a, PACK], BF16, name="woven%d" % a, align_bytes=64) for a, b in PIECES]
-        for piece, (a, b) in enumerate(PIECES):
-            (nc.scalar.copy, nc.vector.tensor_copy)[piece % 2](*woven_views(woven[piece][:], found, a, b))
+        woven = keep.tile([P, V, PACK], BF16, name="woven", align_bytes=64)
+        for copy, a, b in (
+            (nc.scalar.copy, 0, P),
+            (nc.vector.tensor_copy, WEAVE_CUT, V),
+            (nc.scalar.copy, P, V // 2),
+            (nc.scalar.copy, V // 2, WEAVE_CUT),
+        ):
+            copy(*woven_views(woven[:, a:b, :], found, a, b))
 
+        totals = []
         for piece, (a, b) in enumerate(PIECES):
-            codes = keep.tile([P, b - a], U32, name="hc_codes%d" % piece, align_bytes=64)
-            plane = keep.tile([P, b - a], U8, name="hc_plane%d" % piece, align_bytes=64)
-            quantise(woven[piece], codes[:], plane[:])
-            total = bank(piece)
+            totals.append(bank(piece)[:, : b - a])
             nc.tensor.matmul_mx(
-                out=total[:, : b - a],
+                out=totals[piece],
                 lhsT=w3_codes[:].bitcast(FP4X4),
                 lhsT_scale=w3_plane[:],
                 rhs=z_codes[:, a:b].bitcast(FP8X4),
@@ -223,8 +226,12 @@ def tile_picked_sagecat_mean_p_kernel(
                 start=True,
                 stop=False,
             )
+        for piece, (a, b) in enumerate(PIECES):
+            codes = keep.tile([P, b - a], U32, name="hc_codes%d" % piece, align_bytes=64)
+            plane = keep.tile([P, b - a], U8, name="hc_plane%d" % piece, align_bytes=64)
+            quantise(woven[:, a:b, :], codes[:], plane[:])
             nc.tensor.matmul_mx(
-                out=total[:, : b - a],
+                out=totals[piece],
                 lhsT=w2_codes[:].bitcast(FP4X4),
                 lhsT_scale=w2_plane[:],
                 rhs=codes[:].bitcast(FP8X4),
@@ -233,8 +240,8 @@ def tile_picked_sagecat_mean_p_kernel(
                 stop=True,
             )
             result = keep.tile([P, b - a], F32, name="result%d" % piece, align_bytes=64)
-            if piece == 1:
-                nc.vector.tensor_copy(result[:], total[:, : b - a])
+            if piece == 2:
+                nc.vector.tensor_copy(result[:], totals[piece])
             else:
-                nc.scalar.copy(result[:], total[:, : b - a])
-            nc.sync.dma_start(out=out[:, a:b], in_=result[:])
+                nc.scalar.copy(result[:], totals[piece])
+            (nc.scalar if piece == 3 else nc.sync).dma_start(out=out[:, a:b], in_=result[:])

@@ -19,14 +19,17 @@ ADD = mybir.AluOpType.add
 
 P = 128
 PACK = 4
+BANK = 512
 LIST_ROWS = 16
 NEIGHBOURS = 3
 ROW_STEP = P // 16
 ROW_FIRST = 4
-WORD_PIECES = ((0, 256), (256, 768), (768, 1024))
-HALVES = ((0, 256), (256, 512))
-PIECES = ((0, 128), (128, 256), (384, 512), (256, 384))
-WEAVE_CUT = 320
+EDGE = S // 4
+WORD_PIECES = ((0, EDGE), (EDGE, S - EDGE), (S - EDGE, S))
+H0_PARTS = ((256, 512), (512, 768), (768, 896), (896, 1024))
+HALVES = ((0, V // 2), (V // 2, V))
+BLOCKS = ((0, 128), (128, 256), (384, 512), (256, 384))
+WEAVE_CUT = 352
 
 
 def tile_picked_sagecat_mean_p_kernel(
@@ -82,11 +85,13 @@ def tile_picked_sagecat_mean_p_kernel(
         nc.scalar.copy(
             w1_bf[:].rearrange("p t q j -> p q t j"), w1_raw[:].rearrange("p j (q t) -> p q t j", t=PACK)
         )
+
+        def quantise(src, codes, plane):
+            nc.vector.quantize_mx(out=codes.bitcast(FP8X4), scales=plane, in_=src.rearrange("p n t -> p (n t)"))
+
         w1_codes = keep.tile([P, H], U32, name="w1_codes", align_bytes=64)
         w1_plane = keep.tile([P, H], U8, name="w1_plane", align_bytes=64)
-        nc.vector.quantize_mx(
-            out=w1_codes[:].bitcast(FP8X4), scales=w1_plane[:], in_=w1_bf[:].rearrange("p t m j -> p (t m j)")
-        )
+        quantise(w1_bf[:].rearrange("p t q j -> p (t q) j"), w1_codes[:], w1_plane[:])
 
         words = []
         for a, b in WORD_PIECES:
@@ -95,19 +100,19 @@ def tile_picked_sagecat_mean_p_kernel(
             words.append(tile)
 
         def bank(number):
-            return psum.tile([P, 512], F32, name="bank", tag="bank%d" % number)
+            return psum.tile([P, BANK], F32, name="bank", tag="bank%d" % number)
 
         h = [keep.tile([P, S], F32, name="h%d" % t, align_bytes=64) for t in range(PACK)]
 
         def product(t, acc, a, b):
-            piece = max(i for i, (c, d) in enumerate(WORD_PIECES) if c <= a)
-            first = WORD_PIECES[piece][0]
+            piece = max(i for i, (start, end) in enumerate(WORD_PIECES) if start <= a)
+            start = WORD_PIECES[piece][0]
             cols = slice(t * P, (t + 1) * P)
             nc.tensor.matmul_mx(
                 out=acc,
                 lhsT=w1_codes[:, cols].bitcast(FP8X4),
                 lhsT_scale=w1_plane[:, cols],
-                rhs=words[piece][:, a - first : b - first].bitcast(FP8X4),
+                rhs=words[piece][:, a - start : b - start].bitcast(FP8X4),
                 rhs_scale=picked_plane[:, a:b],
                 start=True,
                 stop=True,
@@ -119,106 +124,100 @@ def tile_picked_sagecat_mean_p_kernel(
             else:
                 nc.vector.tensor_scalar_max(h[t][:, a:b], acc, 0.0)
 
-        def gather(on_scalar, dst, window, offsets):
-            if on_scalar:
-                nc.scalar.activation(dst, window.indirect(offsets), COPY)
-            else:
-                nc.vector.tensor_copy(dst, window.indirect(offsets))
+        def gather_on_scalar(dst, window, offsets):
+            nc.scalar.activation(dst, window.indirect(offsets), COPY)
 
-        narrow = [bank(t) for t in range(PACK)]
+        edge_banks = [bank(t) for t in range(PACK)]
         for t in range(PACK):
-            product(t, narrow[t][:, :256], 0, 256)
-        for t in range(3):
-            relu(True, t, narrow[t][:, :256], 0, 256)
-        relu(False, 3, narrow[3][:, :256], 0, 256)
-        for part, (a, b) in enumerate(((256, 512), (512, 768), (768, 896), (896, 1024))):
+            product(t, edge_banks[t][:, :EDGE], 0, EDGE)
+        for t in range(PACK):
+            relu(t < PACK - 1, t, edge_banks[t][:, :EDGE], 0, EDGE)
+        for part, (a, b) in enumerate(H0_PARTS):
             acc = bank(PACK + part)
             product(0, acc[:, : b - a], a, b)
-            relu(part < 3, 0, acc[:, : b - a], a, b)
+            relu(part < len(H0_PARTS) - 1, 0, acc[:, : b - a], a, b)
 
         sums = keep.tile([P, PACK, V], F32, name="sums", align_bytes=64)
         ones = [keep.tile([P, V], F32, name="one%d" % t, align_bytes=64) for t in range(PACK)]
-        gather(False, ones[0][:, : V // 2], h[0][:], entries(pos_lists[0], 0, V // 2))
-        gather(True, ones[0][:, V // 2 :], h[0][:], entries(pos_lists[0], V // 2, V))
-        wide = [None]
+        nc.vector.tensor_copy(ones[0][:, : V // 2], h[0][:].indirect(entries(pos_lists[0], 0, V // 2)))
+        gather_on_scalar(ones[0][:, V // 2 :], h[0][:], entries(pos_lists[0], V // 2, V))
+
+        middle_banks = {}
         for t in range(1, PACK):
-            wide.append(bank(PACK + t - 1))
-            product(t, wide[t][:], 256, 768)
-            product(t, narrow[t][:, 256:], 768, 1024)
+            middle_banks[t] = bank(PACK + t - 1)
+            product(t, middle_banks[t][:], EDGE, S - EDGE)
+            product(t, edge_banks[t][:, EDGE:], S - EDGE, S)
 
-        def rest(t, part):
-            if part == 0:
-                relu(True, t, wide[t][:], 256, 768)
-            else:
-                relu(True, t, narrow[t][:, 256:], 768, 1024)
+        def relu_middle(t):
+            relu(True, t, middle_banks[t][:], EDGE, S - EDGE)
 
-        def first(t):
-            gather(True, ones[t][:, :], h[t][:], pos_lists[0][:])
+        def relu_last(t):
+            relu(True, t, edge_banks[t][:, EDGE:], S - EDGE, S)
 
-        rest(1, 0)
-        rest(1, 1)
-        rest(2, 0)
-        first(1)
-        rest(2, 1)
-        rest(3, 0)
-        rest(3, 1)
-        first(2)
-        first(3)
+        def first_neighbours(t):
+            gather_on_scalar(ones[t][:], h[t][:], pos_lists[0][:])
+
+        relu_middle(1)
+        relu_last(1)
+        relu_middle(2)
+        first_neighbours(1)
+        relu_last(2)
+        relu_middle(3)
+        relu_last(3)
+        first_neighbours(2)
+        first_neighbours(3)
 
         twos = [keep.tile([P, V], F32, name="two%d" % t, align_bytes=64) for t in range(PACK)]
 
-        def add(t, d, a, b):
+        def add_neighbour(t, d, a, b):
             src, dst = ((ones[t], twos[t]), (twos[t], sums[:, t, :]))[d - 1]
             nc.vector.tensor_tensor(dst[:, a:b], h[t][:].indirect(entries(pos_lists[d], a, b)), src[:, a:b], ADD)
 
         for t in (0, 1):
-            for d in (1, 2):
+            for d in range(1, NEIGHBOURS):
                 for a, b in reversed(HALVES) if t == 0 else HALVES:
-                    add(t, d, a, b)
-        add(2, 1, 0, V)
-        add(3, 1, 0, V)
-        add(2, 2, 0, V)
+                    add_neighbour(t, d, a, b)
+        add_neighbour(2, 1, 0, V)
+        add_neighbour(3, 1, 0, V)
+        add_neighbour(2, 2, 0, V)
         for a, b in HALVES:
-            add(3, 2, a, b)
+            add_neighbour(3, 2, a, b)
 
-        found = keep.tile([P, PACK, V], F32, name="found", align_bytes=64)
-        for slot in range(PACK):
-            gather(True, found[:, slot, :], h[slot][:], cen_list[:])
+        centres = keep.tile([P, PACK, V], F32, name="centres", align_bytes=64)
+        for t in range(PACK):
+            gather_on_scalar(centres[:, t, :], h[t][:], cen_list[:])
 
-        def woven_views(tile, src, a, b):
+        def woven_views(dst, src, a, b):
             return (
-                tile.rearrange("p (c n) t -> p c t n", n=4),
+                dst.rearrange("p (c n) t -> p c t n", n=4),
                 src[:, :, a:b].rearrange("p t (c n) -> p c t n", n=4),
             )
 
-        def quantise(tile, codes, plane):
-            nc.vector.quantize_mx(out=codes.bitcast(FP8X4), scales=plane, in_=tile.rearrange("p n t -> p (n t)"))
-
         z_codes = keep.tile([P, V], U32, name="z_codes", align_bytes=64)
         z_plane = keep.tile([P, V], U8, name="z_plane", align_bytes=64)
-        z_bf = []
-        for half in range(2):
-            tile = keep.tile([P, V // 2, PACK], BF16, name="z_bf%d" % half, align_bytes=64)
-            nc.vector.tensor_scalar_mul(*woven_views(tile[:], sums, half * V // 2, (half + 1) * V // 2), 1.0 / NEIGHBOURS)
-            z_bf.append(tile)
-        for half in range(2):
-            cols = slice(half * V // 2, (half + 1) * V // 2)
-            quantise(z_bf[half][:], z_codes[:, cols], z_plane[:, cols])
+        z_halves = []
+        for a, b in HALVES:
+            tile = keep.tile([P, b - a, PACK], BF16, name="z_bf%d" % a, align_bytes=64)
+            nc.vector.tensor_scalar_mul(*woven_views(tile[:], sums, a, b), 1.0 / NEIGHBOURS)
+            z_halves.append(tile)
+        for tile, (a, b) in zip(z_halves, HALVES):
+            quantise(tile[:], z_codes[:, a:b], z_plane[:, a:b])
 
-        woven = keep.tile([P, V, PACK], BF16, name="woven", align_bytes=64)
+        centres_bf = keep.tile([P, V, PACK], BF16, name="centres_bf", align_bytes=64)
         for copy, a, b in (
             (nc.scalar.copy, 0, P),
             (nc.vector.tensor_copy, WEAVE_CUT, V),
-            (nc.scalar.copy, P, V // 2),
-            (nc.scalar.copy, V // 2, WEAVE_CUT),
+            (nc.scalar.copy, P, 2 * P),
+            (nc.scalar.copy, 2 * P, WEAVE_CUT),
         ):
-            copy(*woven_views(woven[:, a:b, :], found, a, b))
+            copy(*woven_views(centres_bf[:, a:b, :], centres, a, b))
 
-        totals = []
-        for piece, (a, b) in enumerate(PIECES):
-            totals.append(bank(piece)[:, : b - a])
+        totals = [bank(block)[:, : b - a] for block, (a, b) in enumerate(BLOCKS)]
+
+        def open_sum(block):
+            a, b = BLOCKS[block]
             nc.tensor.matmul_mx(
-                out=totals[piece],
+                out=totals[block],
                 lhsT=w3_codes[:].bitcast(FP4X4),
                 lhsT_scale=w3_plane[:],
                 rhs=z_codes[:, a:b].bitcast(FP8X4),
@@ -226,12 +225,14 @@ def tile_picked_sagecat_mean_p_kernel(
                 start=True,
                 stop=False,
             )
-        for piece, (a, b) in enumerate(PIECES):
-            codes = keep.tile([P, b - a], U32, name="hc_codes%d" % piece, align_bytes=64)
-            plane = keep.tile([P, b - a], U8, name="hc_plane%d" % piece, align_bytes=64)
-            quantise(woven[:, a:b, :], codes[:], plane[:])
+
+        def close_sum(block):
+            a, b = BLOCKS[block]
+            codes = keep.tile([P, b - a], U32, name="centre_codes%d" % block, align_bytes=64)
+            plane = keep.tile([P, b - a], U8, name="centre_plane%d" % block, align_bytes=64)
+            quantise(centres_bf[:, a:b, :], codes[:], plane[:])
             nc.tensor.matmul_mx(
-                out=totals[piece],
+                out=totals[block],
                 lhsT=w2_codes[:].bitcast(FP4X4),
                 lhsT_scale=w2_plane[:],
                 rhs=codes[:].bitcast(FP8X4),
@@ -239,9 +240,17 @@ def tile_picked_sagecat_mean_p_kernel(
                 start=False,
                 stop=True,
             )
-            result = keep.tile([P, b - a], F32, name="result%d" % piece, align_bytes=64)
-            if piece == 2:
-                nc.vector.tensor_copy(result[:], totals[piece])
-            else:
-                nc.scalar.copy(result[:], totals[piece])
-            (nc.scalar if piece == 3 else nc.sync).dma_start(out=out[:, a:b], in_=result[:])
+            last = len(BLOCKS) - 1
+            result = keep.tile([P, b - a], F32, name="result%d" % block, align_bytes=64)
+            copy = nc.scalar.copy if block in (0, last) else nc.vector.tensor_copy
+            copy(result[:], totals[block])
+            queue = nc.scalar if block == last else nc.sync
+            queue.dma_start(out=out[:, a:b], in_=result[:])
+
+        open_sum(0)
+        open_sum(1)
+        close_sum(0)
+        open_sum(2)
+        open_sum(3)
+        for block in range(1, len(BLOCKS)):
+            close_sum(block)

@@ -22,8 +22,7 @@ PACK = 4
 BANK = 512
 LIST_ROWS = 16
 NEIGHBOURS = 3
-ROW_STEP = P // 16
-ROW_FIRST = 4
+ROW_FIRST, ROW_END, ROW_STEP = 32, 96, 4
 EDGE = S // 4
 WORD_PIECES = ((0, EDGE), (EDGE, S - EDGE), (S - EDGE, S))
 H0_PARTS = ((256, 512), (512, 768), (768, 896), (896, 1024))
@@ -64,13 +63,13 @@ def tile_picked_sagecat_mean_p_kernel(
         w1_raw = keep.tile([P, PACK, H], F32, name="w1_raw")
         nc.sync.dma_start(out=w1_raw[:], in_=w1.rearrange("(p j) c -> p j c", j=PACK))
         offs_list = load_list("offs_list", offs)
-        nc.sync.dma_start(out=x_rows[ROW_FIRST:P:ROW_STEP, :].bitcast(I32), in_=x_scales[0].bitcast(I32))
+        nc.sync.dma_start(out=x_rows[ROW_FIRST:ROW_END:ROW_STEP, :].bitcast(I32), in_=x_scales[0].bitcast(I32))
         x_table = keep.tile([P, T], U32, name="x_table")
         nc.sync.dma_start(out=x_table[:].bitcast(I32), in_=x_words[0].rearrange("p n t -> p (n t)").bitcast(I32))
 
         picked_rows = keep.tile([P, S], U8, name="picked_rows")
         nc.vector.tensor_copy(picked_rows[:], x_rows[:].indirect(offs_list[:]))
-        place_scale_rows(picked_plane, lambda r: picked_rows[ROW_FIRST + ROW_STEP * r : P : 32, :])
+        place_scale_rows(picked_plane, lambda r: picked_rows[ROW_FIRST + ROW_STEP * r : ROW_END : 4 * ROW_STEP, :])
 
         pos_lists = [load_list("pos%d_list" % d, src) for d, src in enumerate((pos1, pos2, pos3))]
         cen_list = load_list("cen_list", cen)

from contextlib import ExitStack

import concourse.mybir as mybir

K, T, S, V, H, N = 512, 4096, 1024, 512, 512, 128
FLOPS = 2 * K * H * S + 2 * 2 * H * N * V

F32 = mybir.dt.float32
BF16 = mybir.dt.bfloat16
I32 = mybir.dt.int32
U32 = mybir.dt.uint32
U16 = mybir.dt.uint16
U8 = mybir.dt.uint8
FP8X4 = mybir.dt.float8_e4m3fn_x4
FP4X4 = mybir.dt.float4_e2m1fn_x4
COPY = mybir.ActivationFunctionType.Copy
RELU = mybir.ActivationFunctionType.Relu
ADD = mybir.AluOpType.add

P = 128
PACK = 4
BANK = 512
LIST_ROWS = 16
NEIGHBOURS = 3
ROW_FIRST, ROW_END, ROW_STEP = 32, 96, 4
EDGE = S // 4
WORD_PIECES = ((0, EDGE), (EDGE, S - EDGE), (S - EDGE, S))
H0_PARTS = ((256, 512), (512, 768), (768, 896), (896, 1024))
HALVES = ((0, V // 2), (V // 2, V))
BLOCKS = ((0, 128), (128, 256), (384, 512), (256, 384))
WEAVE_CUT = 352


def tile_picked_sagecat_mean_p_kernel(
    tc, x_words, x_scales, w1, w2_words, w2_scales, w3_words, w3_scales, offs, cen, pos1, pos2, pos3, out
):
    nc = tc.nc
    with ExitStack() as ctx:
        keep = ctx.enter_context(tc.tile_pool(name="keep", bufs=1))
        psum = ctx.enter_context(tc.psum_pool(name="psum", bufs=1))

        def load_list(name, src):
            tile = keep.tile(list(src.shape), U16, name=name)
            nc.sync.dma_start(tile[:], src)
            return tile

        def entries(list_tile, a, b):
            return list_tile[:, a // LIST_ROWS : b // LIST_ROWS]

        def place_scale_rows(plane, rows):
            for r in range(4):
                nc.sync.dma_start(out=plane[r:P:32, :].bitcast(I32), in_=rows(r).bitcast(I32))

        x_rows = keep.tile([P, T], U8, name="x_rows")
        nc.vector.memset(x_rows[:].bitcast(I32), 0)
        picked_plane = keep.tile([P, S], U8, name="picked_plane", align_bytes=64)
        nc.vector.memset(picked_plane[:].bitcast(I32), 0)
        w2_plane = keep.tile([P, N], U8, name="w2_plane", align_bytes=64)
        w3_plane = keep.tile([P, N], U8, name="w3_plane", align_bytes=64)
        nc.vector.memset(w2_plane[:].bitcast(I32), 0)
        nc.vector.memset(w3_plane[:].bitcast(I32), 0)

        w1_raw = keep.tile([P, PACK, H], F32, name="w1_raw")
        nc.sync.dma_start(out=w1_raw[:], in_=w1.rearrange("(p j) c -> p j c", j=PACK))
        offs_list = load_list("offs_list", offs)
        nc.sync.dma_start(out=x_rows[ROW_FIRST:ROW_END:ROW_STEP, :].bitcast(I32), in_=x_scales[0].bitcast(I32))
        x_table = keep.tile([P, T], U32, name="x_table")
        nc.sync.dma_start(out=x_table[:].bitcast(I32), in_=x_words[0].rearrange("p n t -> p (n t)").bitcast(I32))

        picked_rows = keep.tile([P, S], U8, name="picked_rows")
        nc.vector.tensor_copy(picked_rows[:], x_rows[:].indirect(offs_list[:]))
        place_scale_rows(picked_plane, lambda r: picked_rows[ROW_FIRST + ROW_STEP * r : ROW_END : 4 * ROW_STEP, :])

        pos_lists = [load_list("pos%d_list" % d, src) for d, src in enumerate((pos1, pos2, pos3))]
        cen_list = load_list("cen_list", cen)
        w2_codes = keep.tile([P, 2 * N], U8, name="w2_codes", align_bytes=64)
        w3_codes = keep.tile([P, 2 * N], U8, name="w3_codes", align_bytes=64)
        nc.sync.dma_start(out=w3_codes[:].bitcast(I32), in_=w3_words[0].bitcast(I32))
        nc.sync.dma_start(out=w2_codes[:].bitcast(I32), in_=w2_words[0].bitcast(I32))
        place_scale_rows(w3_plane, lambda r: w3_scales[0, r:16:4, :])
        place_scale_rows(w2_plane, lambda r: w2_scales[0, r:16:4, :])

        w1_bf = keep.tile([P, PACK, P, PACK], BF16, name="w1_bf", align_bytes=64)
        nc.scalar.copy(
            w1_bf[:].rearrange("p t q j -> p q t j"), w1_raw[:].rearrange("p j (q t) -> p q t j", t=PACK)
        )

        def quantise(src, codes, plane):
            nc.vector.quantize_mx(out=codes.bitcast(FP8X4), scales=plane, in_=src.rearrange("p n t -> p (n t)"))

        w1_codes = keep.tile([P, H], U32, name="w1_codes", align_bytes=64)
        w1_plane = keep.tile([P, H], U8, name="w1_plane", align_bytes=64)
        quantise(w1_bf[:].rearrange("p t q j -> p (t q) j"), w1_codes[:], w1_plane[:])

        words = []
        for a, b in WORD_PIECES:
            tile = keep.tile([P, b - a], U32, name="words%d" % a, align_bytes=64)
            nc.vector.tensor_copy(tile[:], x_table[:].indirect(entries(offs_list, a, b)))
            words.append(tile)

        def bank(number):
            return psum.tile([P, BANK], F32, name="bank", tag="bank%d" % number)

        h = [keep.tile([P, S], F32, name="h%d" % t, align_bytes=64) for t in range(PACK)]

        def product(t, acc, a, b):
            piece = max(i for i, (start, end) in enumerate(WORD_PIECES) if start <= a)
            start = WORD_PIECES[piece][0]
            cols = slice(t * P, (t + 1) * P)
            nc.tensor.matmul_mx(
                out=acc,
                lhsT=w1_codes[:, cols].bitcast(FP8X4),
                lhsT_scale=w1_plane[:, cols],
                rhs=words[piece][:, a - start : b - start].bitcast(FP8X4),
                rhs_scale=picked_plane[:, a:b],
                start=True,
                stop=True,
            )

        def relu(on_scalar, t, acc, a, b):
            if on_scalar:
                nc.scalar.activation(h[t][:, a:b], acc, RELU)
            else:
                nc.vector.tensor_scalar_max(h[t][:, a:b], acc, 0.0)

        def gather_on_scalar(dst, window, offsets):
            nc.scalar.activation(dst, window.indirect(offsets), COPY)

        edge_banks = [bank(t) for t in range(PACK)]
        for t in range(PACK):
            product(t, edge_banks[t][:, :EDGE], 0, EDGE)
        for t in range(PACK):
            relu(t < PACK - 1, t, edge_banks[t][:, :EDGE], 0, EDGE)
        for part, (a, b) in enumerate(H0_PARTS):
            acc = bank(PACK + part)
            product(0, acc[:, : b - a], a, b)
            relu(part < len(H0_PARTS) - 1, 0, acc[:, : b - a], a, b)

        sums = keep.tile([P, PACK, V], F32, name="sums", align_bytes=64)
        ones = [keep.tile([P, V], F32, name="one%d" % t, align_bytes=64) for t in range(PACK)]
        nc.vector.tensor_copy(ones[0][:, : V // 2], h[0][:].indirect(entries(pos_lists[0], 0, V // 2)))
        gather_on_scalar(ones[0][:, V // 2 :], h[0][:], entries(pos_lists[0], V // 2, V))

        middle_banks = {}
        for t in range(1, PACK):
            middle_banks[t] = bank(PACK + t - 1)
            product(t, middle_banks[t][:], EDGE, S - EDGE)
            product(t, edge_banks[t][:, EDGE:], S - EDGE, S)

        def relu_middle(t):
            relu(True, t, middle_banks[t][:], EDGE, S - EDGE)

        def relu_last(t):
            relu(True, t, edge_banks[t][:, EDGE:], S - EDGE, S)

        def first_neighbours(t):
            gather_on_scalar(ones[t][:], h[t][:], pos_lists[0][:])

        relu_middle(1)
        relu_last(1)
        relu_middle(2)
        first_neighbours(1)
        relu_last(2)
        relu_middle(3)
        relu_last(3)
        first_neighbours(2)
        first_neighbours(3)

        twos = [keep.tile([P, V], F32, name="two%d" % t, align_bytes=64) for t in range(PACK)]

        def add_neighbour(t, d, a, b):
            src, dst = ((ones[t], twos[t]), (twos[t], sums[:, t, :]))[d - 1]
            nc.vector.tensor_tensor(dst[:, a:b], h[t][:].indirect(entries(pos_lists[d], a, b)), src[:, a:b], ADD)

        for t in (0, 1):
            for d in range(1, NEIGHBOURS):
                for a, b in reversed(HALVES) if t == 0 else HALVES:
                    add_neighbour(t, d, a, b)
        add_neighbour(2, 1, 0, V)
        add_neighbour(3, 1, 0, V)
        add_neighbour(2, 2, 0, V)
        for a, b in HALVES:
            add_neighbour(3, 2, a, b)

        centres = keep.tile([P, PACK, V], F32, name="centres", align_bytes=64)
        for t in range(PACK):
            gather_on_scalar(centres[:, t, :], h[t][:], cen_list[:])

        def woven_views(dst, src, a, b):
            return (
                dst.rearrange("p (c n) t -> p c t n", n=4),
                src[:, :, a:b].rearrange("p t (c n) -> p c t n", n=4),
            )

        z_codes = keep.tile([P, V], U32, name="z_codes", align_bytes=64)
        z_plane = keep.tile([P, V], U8, name="z_plane", align_bytes=64)
        z_halves = []
        for a, b in HALVES:
            tile = keep.tile([P, b - a, PACK], BF16, name="z_bf%d" % a, align_bytes=64)
            nc.vector.tensor_scalar_mul(*woven_views(tile[:], sums, a, b), 1.0 / NEIGHBOURS)
            z_halves.append(tile)
        for tile, (a, b) in zip(z_halves, HALVES):
            quantise(tile[:], z_codes[:, a:b], z_plane[:, a:b])

        centres_bf = keep.tile([P, V, PACK], BF16, name="centres_bf", align_bytes=64)
        for copy, a, b in (
            (nc.scalar.copy, 0, P),
            (nc.vector.tensor_copy, WEAVE_CUT, V),
            (nc.scalar.copy, P, 2 * P),
            (nc.scalar.copy, 2 * P, WEAVE_CUT),
        ):
            copy(*woven_views(centres_bf[:, a:b, :], centres, a, b))

        totals = [bank(block)[:, : b - a] for block, (a, b) in enumerate(BLOCKS)]

        def open_sum(block):
            a, b = BLOCKS[block]
            nc.tensor.matmul_mx(
                out=totals[block],
                lhsT=w3_codes[:].bitcast(FP4X4),
                lhsT_scale=w3_plane[:],
                rhs=z_codes[:, a:b].bitcast(FP8X4),
                rhs_scale=z_plane[:, a:b],
                start=True,
                stop=False,
            )

        def close_sum(block):
            a, b = BLOCKS[block]
            codes = keep.tile([P, b - a], U32, name="centre_codes%d" % block, align_bytes=64)
            plane = keep.tile([P, b - a], U8, name="centre_plane%d" % block, align_bytes=64)
            quantise(centres_bf[:, a:b, :], codes[:], plane[:])
            nc.tensor.matmul_mx(
                out=totals[block],
                lhsT=w2_codes[:].bitcast(FP4X4),
                lhsT_scale=w2_plane[:],
                rhs=codes[:].bitcast(FP8X4),
                rhs_scale=plane[:],
                start=False,
                stop=True,
            )
            last = len(BLOCKS) - 1
            result = keep.tile([P, b - a], F32, name="result%d" % block, align_bytes=64)
            copy = nc.scalar.copy if block in (0, last) else nc.vector.tensor_copy
            copy(result[:], totals[block])
            queue = nc.scalar if block == last else nc.sync
            queue.dma_start(out=out[:, a:b], in_=result[:])

        open_sum(0)
        open_sum(1)
        close_sum(0)
        open_sum(2)
        open_sum(3)
        for block in range(1, len(BLOCKS)):
            close_sum(block)
